import numpy as np
import ml_dtypes


def mxq(x, axis, fmt="e4m3"):
    dtype, down = {"e4m3": (ml_dtypes.float8_e4m3fn, 7), "e5m2": (ml_dtypes.float8_e5m2, 14)}[fmt]
    v = np.moveaxis(np.asarray(x, np.float32).astype(ml_dtypes.bfloat16).astype(np.float64), axis, -1)
    blocks = v.reshape(v.shape[:-1] + (-1, 32))
    amax = np.abs(blocks).max(-1, keepdims=True)
    byte = np.maximum(np.where(amax > 0, np.frexp(amax)[1] - 1 + 127, 0) - down, 1)
    scale = np.exp2(byte - 127.0)
    codes = (blocks / scale).astype(np.float32).astype(dtype).astype(np.float64)
    return np.moveaxis((codes * scale).reshape(v.shape), -1, axis)


WIDE = False


def mx_kscale(k):
    if not WIDE:
        return np.ones(k)
    levels = np.array([10, -10, 5, -5, 0])
    if k % 512:
        return np.exp2(np.random.permutation(np.resize(levels, k // 32))).repeat(32)
    a = np.empty((k // 512, 16))
    for p in range(k // 512):
        a[p, :8] = np.random.permutation(np.resize(levels, 8))
        for g in range(8):
            far = levels[np.abs(levels - a[p, g]) >= 10]
            a[p, g + 8] = far[np.random.randint(len(far))]
    return np.exp2(a.ravel()).repeat(32)


def f64(x):
    return np.asarray(x).astype(np.float64)


def striped(idx):
    return np.tile(idx.reshape(-1, 16).T, (8, 1)).astype(np.uint16)


def unstriped(offs):
    return offs[:16].T.reshape(-1).astype(np.int64)


def relu(v):
    return np.maximum(v, 0.0)


K, T, E, C, H, N = 1024, 1024, 2, 256, 512, 128


def by_expert(wq, xq):
    return np.concatenate([wq[e].T @ xq[:, e * C:(e + 1) * C] for e in range(E)], axis=1)


def setup_inputs():
    n = np.random.standard_normal
    s = mx_kscale(K)[:, None]
    u = mx_kscale(H)
    return {
        "xT": (n((K, T)) * s).astype(np.float32),
        "xr": n((N, T)).astype(np.float32),
        "w1": (n((E, K, H)) / np.sqrt(K) / s[None]).astype(np.float32),
        "w3": (n((E, K, H)) / np.sqrt(K) / s[None] * u[None, None, :]).astype(np.float32),
        "w2": (n((E, H, N)) / np.sqrt(H) / u[None, :, None]).astype(np.float32),
        "gate": np.tile(np.random.uniform(0.2, 1.0, E * C), (N, 1)).astype(np.float32),
        "offs": striped(np.random.permutation(T)[:E * C]),
    }


def reference(xT, xr, w1, w3, w2, gate, offs):
    idx = unstriped(offs)
    xq = mxq(f64(xT)[:, idx], 0, "e4m3")
    h = relu(by_expert(mxq(f64(w1), 1, "e4m3"), xq))
    h = h * by_expert(mxq(f64(w3), 1, "e4m3"), xq)
    y = by_expert(mxq(f64(w2), 1, "e4m3"), mxq(h, 0, "e4m3"))
    out = f64(xr).copy()
    out[:, idx] += f64(gate) * y
    return out

@@ -1,0 +1,284 @@
+from contextlib import ExitStack
+
+import concourse.mybir as mybir
+
+K, T, E, C, H, N = 1024, 1024, 2, 256, 512, 128
+S = E * C
+FLOPS = 2 * S * (2 * K * H + H * N)
+
+P = 128
+PACK = 4
+K_PASS = P * PACK
+PASSES = K // K_PASS
+BLK = 128
+HALF = T // 2
+
+F32 = mybir.dt.float32
+BF16 = mybir.dt.bfloat16
+U32 = mybir.dt.uint32
+U16 = mybir.dt.uint16
+U8 = mybir.dt.uint8
+FP8X4 = mybir.dt.float8_e4m3fn_x4
+COPY = mybir.ActivationFunctionType.Copy
+RELU = mybir.ActivationFunctionType.Relu
+MULT = mybir.AluOpType.mult
+ADD = mybir.AluOpType.add
+
+
+def tile_moe_res_glu_relu_kernel(tc, xT, xr, w1, w3, w2, gate, offs, out):
+    nc = tc.nc
+    with ExitStack() as ctx:
+        keep = ctx.enter_context(tc.tile_pool(name="keep", bufs=1))
+        psum = ctx.enter_context(tc.psum_pool(name="psum", bufs=6))
+        psum_y = ctx.enter_context(tc.psum_pool(name="psum_y", bufs=2))
+
+        offsets = keep.tile([P, S // 16], U16, name="offsets")
+
+        x_raw = {}
+        x_bf = {}
+        for s in range(PASSES):
+            x_raw[s] = keep.tile([P, PACK, T], F32, name=f"x_raw{s}")
+            x_bf[s] = keep.tile([P, T * PACK], BF16, name=f"x_bf{s}", align_bytes=64)
+        x_words = [keep.tile([P, T], U32, name=f"x_words{s}", align_bytes=64) for s in range(PASSES)]
+        x_bytes = keep.tile([P, T], U8, name="x_bytes", align_bytes=64)
+        slot_words = [keep.tile([P, S], U32, name=f"slot_words{s}", align_bytes=64) for s in range(PASSES)]
+        slot_bytes = keep.tile([P, S], U8, name="slot_bytes", align_bytes=64)
+        window = keep.tile([P, T], F32, name="window")
+        nc.gpsimd.memset(x_bytes[:], 0)
+        nc.gpsimd.memset(window[:], 0.0)
+
+        w_raw, w_bf, w_codes, w_scales = {}, {}, {}, {}
+        for e in range(E):
+            for g in range(2):
+                for s in range(PASSES):
+                    key = (e, g, s)
+                    w_raw[key] = keep.tile([P, PACK, H], F32, name=f"w_raw{e}{g}{s}")
+                    w_bf[key] = keep.tile([P, H * PACK], BF16, name=f"w_bf{e}{g}{s}", align_bytes=64)
+                    w_codes[key] = keep.tile([P, H], U32, name=f"w_codes{e}{g}{s}", align_bytes=64)
+                    w_scales[key] = keep.tile([P, H], U8, name=f"w_scales{e}{g}{s}", align_bytes=64)
+        w2_raw = [keep.tile([P, PACK, N], F32, name=f"w2_raw{e}") for e in range(E)]
+        w2_bf = [keep.tile([P, N, PACK], BF16, name=f"w2_bf{e}", align_bytes=64) for e in range(E)]
+        w2_codes = [keep.tile([P, N], U32, name=f"w2_codes{e}", align_bytes=64) for e in range(E)]
+        w2_scales = [keep.tile([P, N], U8, name=f"w2_scales{e}", align_bytes=64) for e in range(E)]
+        gate_sb = keep.tile([P, S], F32, name="gate_sb")
+        xr_sb = keep.tile([P, T], F32, name="xr_sb")
+
+        weights = (w1, w3)
+
+        def load_x(s):
+            rows = xT[s * K_PASS : (s + 1) * K_PASS, :]
+            nc.sync.dma_start(x_raw[s][:], rows.rearrange("(p j) w -> p j w", j=PACK))
+
+        def load_w(e, g, s):
+            rows = weights[g][e][s * K_PASS : (s + 1) * K_PASS, :]
+            nc.sync.dma_start(w_raw[e, g, s][:], rows.rearrange("(p j) w -> p j w", j=PACK))
+
+        def load_w2(e):
+            nc.sync.dma_start(w2_raw[e][:], w2[e].rearrange("(p j) n -> p j n", j=PACK))
+
+        load_x(0)
+        nc.sync.dma_start(offsets[:], offs)
+        load_x(1)
+        load_w(0, 0, 0)
+        load_w(0, 0, 1)
+        load_w(0, 1, 0)
+        load_w(0, 1, 1)
+        load_w2(0)
+        load_w(1, 0, 0)
+        load_w(1, 0, 1)
+        load_w(1, 1, 0)
+        load_w(1, 1, 1)
+        load_w2(1)
+        nc.sync.dma_start(gate_sb[:], gate)
+        nc.sync.dma_start(xr_sb[:], xr)
+
+        def cast(dst, src, cut):
+            if cut > 0:
+                nc.scalar.activation(dst[:, :cut], src[:, :cut], COPY)
+            if cut < dst.shape[1]:
+                nc.vector.tensor_copy(dst[:, cut:], src[:, cut:])
+
+        def cast_x(s, h, cut):
+            cols = slice(h * (HALF // 4), (h + 1) * (HALF // 4))
+            dst = x_bf[s][:].rearrange("p (c i t) -> p c t i", i=4, t=PACK)
+            src = x_raw[s][:].rearrange("p t (c i) -> p c t i", i=4)
+            cast(dst[:, cols], src[:, cols], cut)
+
+        def cast_w(e, g, s, cut, lo=0, hi=H // 4):
+            dst = w_bf[e, g, s][:].rearrange("p (t m j) -> p m j t", t=4, j=4)
+            src = w_raw[e, g, s][:].rearrange("p j (m t) -> p m j t", t=4)
+            cast(dst[:, lo:hi], src[:, lo:hi], cut)
+
+        def cast_w2(e, cut):
+            cast(
+                w2_bf[e][:].rearrange("p (c i) t -> p c t i", i=4),
+                w2_raw[e][:].rearrange("p t (c i) -> p c t i", i=4),
+                cut,
+            )
+
+        def quant_x(s, h):
+            cols = slice(h * HALF, (h + 1) * HALF)
+            nc.vector.quantize_mx(
+                out=x_words[s][:, cols].bitcast(FP8X4),
+                scales=x_bytes[4 * s : P, cols],
+                in_=x_bf[s][:, h * HALF * PACK : (h + 1) * HALF * PACK],
+            )
+
+        def quant_w(e, g, s, lo=0, hi=H):
+            nc.vector.quantize_mx(
+                out=w_codes[e, g, s][:, lo:hi].bitcast(FP8X4),
+                scales=w_scales[e, g, s][:, lo:hi],
+                in_=w_bf[e, g, s][:, 4 * lo : 4 * hi],
+            )
+
+        def quant_w2(e):
+            nc.vector.quantize_mx(
+                out=w2_codes[e][:].bitcast(FP8X4),
+                scales=w2_scales[e][:],
+                in_=w2_bf[e][:].rearrange("p w t -> p (w t)"),
+            )
+
+        def product(e, g, b):
+            bank = psum.tile([P, 4, BLK], F32, name="bank")
+            cols = slice(e * C + b * BLK, e * C + (b + 1) * BLK)
+            for t in range(4):
+                for s in range(PASSES):
+                    nc.tensor.matmul_mx(
+                        out=bank[:, t, :],
+                        lhsT=w_codes[e, g, s][:, t * P : (t + 1) * P].bitcast(FP8X4),
+                        lhsT_scale=w_scales[e, g, s][:, t * P : (t + 1) * P],
+                        rhs=slot_words[s][:, cols].bitcast(FP8X4),
+                        rhs_scale=slot_bytes[4 * s : P, cols],
+                        start=(s == 0),
+                        stop=(s == PASSES - 1),
+                    )
+            return bank
+
+        banks, relu_a, h_bf, y_banks = {}, {}, {}, {}
+        h_codes = [keep.tile([P, C], U32, name=f"h_codes{e}", align_bytes=64) for e in range(E)]
+        h_scales = [keep.tile([P, C], U8, name=f"h_scales{e}", align_bytes=64) for e in range(E)]
+        y_sb = [keep.tile([P, C], F32, name=f"y_sb{e}") for e in range(E)]
+
+        def products(e, g):
+            for b in range(2):
+                banks[e, g, b] = product(e, g, b)
+
+        def relu(e, b):
+            relu_a[e, b] = keep.tile([P, BLK, 4], F32, name=f"relu{e}{b}")
+            nc.scalar.activation(relu_a[e, b][:], banks[e, 0, b][:].rearrange("p t n -> p n t"), RELU)
+
+        def hmul(e, b):
+            if b == 0:
+                h_bf[e] = keep.tile([P, C, 4], BF16, name=f"h_bf{e}", align_bytes=64)
+            nc.vector.tensor_tensor(
+                h_bf[e][:, b * BLK : (b + 1) * BLK, :],
+                banks[e, 1, b][:].rearrange("p t n -> p n t"),
+                relu_a[e, b][:],
+                MULT,
+            )
+
+        def down(e, b):
+            if b == 0:
+                y_banks[e] = psum_y.tile([P, C], F32, name="y_bank")
+            cols = slice(b * BLK, (b + 1) * BLK)
+            nc.vector.quantize_mx(
+                out=h_codes[e][:, cols].bitcast(FP8X4),
+                scales=h_scales[e][:, cols],
+                in_=h_bf[e][:, cols, :].rearrange("p n t -> p (n t)"),
+            )
+            nc.tensor.matmul_mx(
+                out=y_banks[e][:, cols],
+                lhsT=w2_codes[e][:].bitcast(FP8X4),
+                lhsT_scale=w2_scales[e][:],
+                rhs=h_codes[e][:, cols].bitcast(FP8X4),
+                rhs_scale=h_scales[e][:, cols],
+                start=True,
+                stop=True,
+            )
+
+        def down_both(e):
+            y_banks[e] = psum_y.tile([P, C], F32, name="y_bank")
+            nc.vector.quantize_mx(
+                out=h_codes[e][:].bitcast(FP8X4),
+                scales=h_scales[e][:],
+                in_=h_bf[e][:].rearrange("p n t -> p (n t)"),
+            )
+            nc.tensor.matmul_mx(
+                out=y_banks[e][:],
+                lhsT=w2_codes[e][:].bitcast(FP8X4),
+                lhsT_scale=w2_scales[e][:],
+                rhs=h_codes[e][:].bitcast(FP8X4),
+                rhs_scale=h_scales[e][:],
+                start=True,
+                stop=True,
+            )
+
+        def ycopy(e, lo=0, hi=C):
+            nc.scalar.activation(y_sb[e][:, lo:hi], y_banks[e][:, lo:hi], COPY)
+
+        def scatter(e, lo, hi):
+            first, last = e * C + lo, e * C + hi
+            nc.vector.tensor_tensor(
+                window[:].indirect(offsets[:, first // 16 : last // 16]),
+                y_sb[e][:, lo:hi],
+                gate_sb[:, first:last],
+                MULT,
+            )
+
+        cast_x(0, 1, 44)
+        quant_x(0, 1)
+        cast_x(0, 0, 64)
+        quant_x(0, 0)
+        nc.vector.tensor_copy(slot_words[0][:], x_words[0][:].indirect(offsets[:]))
+        cast_x(1, 1, 128)
+        cast_x(1, 0, 4)
+        quant_x(1, 0)
+        cast_w(0, 0, 0, 100)
+        quant_x(1, 1)
+        cast_w(0, 0, 1, 116)
+        nc.vector.tensor_copy(slot_words[1][:], x_words[1][:].indirect(offsets[:]))
+        nc.vector.tensor_copy(slot_bytes[:], x_bytes[:].indirect(offsets[:]))
+        quant_w(0, 0, 0)
+        cast_w(0, 1, 0, 128)
+        quant_w(0, 0, 1)
+        cast_w(0, 1, 1, 48)
+        quant_w(0, 1, 0)
+        quant_w(0, 1, 1)
+        products(0, 0)
+        relu(0, 0)
+        products(0, 1)
+        cast_w2(0, 0)
+        quant_w2(0)
+        relu(0, 1)
+        cast_w(1, 0, 0, 84)
+        quant_w(1, 0, 0)
+        hmul(0, 0)
+        hmul(0, 1)
+        cast_w(1, 0, 1, 88)
+        down_both(0)
+        cast_w(1, 1, 0, 28)
+        quant_w(1, 1, 0)
+        quant_w(1, 0, 1)
+        cast_w(1, 1, 1, 36)
+        products(1, 0)
+        quant_w(1, 1, 1)
+        products(1, 1)
+        ycopy(0)
+        relu(1, 0)
+        cast_w2(1, 0)
+        relu(1, 1)
+        scatter(0, 0, C)
+        hmul(1, 0)
+        quant_w2(1)
+        down(1, 0)
+        hmul(1, 1)
+        ycopy(1, 0, 128)
+        scatter(1, 0, BLK)
+        down(1, 1)
+        ycopy(1, 128, 256)
+        scatter(1, BLK, C)
+        for q in range(2):
+            cols = slice(q * HALF, (q + 1) * HALF)
+            out_sb = keep.tile([P, HALF], F32, name=f"out_sb{q}")
+            nc.vector.tensor_tensor(out_sb[:], window[:, cols], xr_sb[:, cols], ADD)
+            nc.sync.dma_start(out[:, cols], out_sb[:])

@@ -29,17 +29,12 @@ def tile_moe_res_glu_relu_kernel(tc, xT, xr, w1, w3, w2, gate, offs, out):
     nc = tc.nc
     with ExitStack() as ctx:
         keep = ctx.enter_context(tc.tile_pool(name="keep", bufs=1))
-        psum = ctx.enter_context(tc.psum_pool(name="psum", bufs=6))
-        psum_y = ctx.enter_context(tc.psum_pool(name="psum_y", bufs=2))
+        psum = ctx.enter_context(tc.psum_pool(name="psum", bufs=8))
 
         offsets = keep.tile([P, S // 16], U16, name="offsets")
 
         x_raw = {}
-        x_bf = {}
-        for s in range(PASSES):
-            x_raw[s] = keep.tile([P, PACK, T], F32, name=f"x_raw{s}")
-            x_bf[s] = keep.tile([P, T * PACK], BF16, name=f"x_bf{s}", align_bytes=64)
-        x_words = [keep.tile([P, T], U32, name=f"x_words{s}", align_bytes=64) for s in range(PASSES)]
+        x_words = [keep.tile([P, T], U32, name=f"x_words{s}", tag=f"x_words{s}", align_bytes=64) for s in range(PASSES)]
         x_bytes = keep.tile([P, T], U8, name="x_bytes", align_bytes=64)
         slot_words = [keep.tile([P, S], U32, name=f"slot_words{s}", align_bytes=64) for s in range(PASSES)]
         slot_bytes = keep.tile([P, S], U8, name="slot_bytes", align_bytes=64)
@@ -47,27 +42,27 @@ def tile_moe_res_glu_relu_kernel(tc, xT, xr, w1, w3, w2, gate, offs, out):
         nc.gpsimd.memset(x_bytes[:], 0)
         nc.gpsimd.memset(window[:], 0.0)
 
-        w_raw, w_bf, w_codes, w_scales = {}, {}, {}, {}
+        w_raw, w_codes, w_scales = {}, {}, {}
         for e in range(E):
             for g in range(2):
                 for s in range(PASSES):
                     key = (e, g, s)
-                    w_raw[key] = keep.tile([P, PACK, H], F32, name=f"w_raw{e}{g}{s}")
-                    w_bf[key] = keep.tile([P, H * PACK], BF16, name=f"w_bf{e}{g}{s}", align_bytes=64)
+                    w_raw[key] = keep.tile([P, PACK, H], F32, name=f"w_raw{e}{g}{s}", tag=f"w_raw{e}{g}{s}", align_bytes=64)
                     w_codes[key] = keep.tile([P, H], U32, name=f"w_codes{e}{g}{s}", align_bytes=64)
                     w_scales[key] = keep.tile([P, H], U8, name=f"w_scales{e}{g}{s}", align_bytes=64)
         w2_raw = [keep.tile([P, PACK, N], F32, name=f"w2_raw{e}") for e in range(E)]
-        w2_bf = [keep.tile([P, N, PACK], BF16, name=f"w2_bf{e}", align_bytes=64) for e in range(E)]
+        w2_bf = {}
         w2_codes = [keep.tile([P, N], U32, name=f"w2_codes{e}", align_bytes=64) for e in range(E)]
         w2_scales = [keep.tile([P, N], U8, name=f"w2_scales{e}", align_bytes=64) for e in range(E)]
-        gate_sb = keep.tile([P, S], F32, name="gate_sb")
+        gate_sb = [keep.tile([P, C], F32, name=f"gate_sb{e}") for e in range(E)]
         xr_sb = keep.tile([P, T], F32, name="xr_sb")
 
         weights = (w1, w3)
 
-        def load_x(s):
-            rows = xT[s * K_PASS : (s + 1) * K_PASS, :]
-            nc.sync.dma_start(x_raw[s][:], rows.rearrange("(p j) w -> p j w", j=PACK))
+        def load_x(s, lo, hi):
+            x_raw[s, lo] = keep.tile([P, PACK, hi - lo], F32, name=f"x_raw{s}_{lo}")
+            rows = xT[s * K_PASS : (s + 1) * K_PASS, lo:hi]
+            nc.sync.dma_start(x_raw[s, lo][:], rows.rearrange("(p j) w -> p j w", j=PACK))
 
         def load_w(e, g, s):
             rows = weights[g][e][s * K_PASS : (s + 1) * K_PASS, :]
@@ -76,59 +71,75 @@ def tile_moe_res_glu_relu_kernel(tc, xT, xr, w1, w3, w2, gate, offs, out):
         def load_w2(e):
             nc.sync.dma_start(w2_raw[e][:], w2[e].rearrange("(p j) n -> p j n", j=PACK))
 
-        load_x(0)
+        def load_gate(e):
+            nc.sync.dma_start(gate_sb[e][:], gate[:, e * C : (e + 1) * C])
+
+        load_x(0, 0, T)
         nc.sync.dma_start(offsets[:], offs)
-        load_x(1)
+        load_x(1, 0, HALF)
+        load_x(1, HALF, T)
         load_w(0, 0, 0)
         load_w(0, 0, 1)
         load_w(0, 1, 0)
         load_w(0, 1, 1)
-        load_w2(0)
         load_w(1, 0, 0)
+        load_w2(0)
         load_w(1, 0, 1)
+        load_gate(0)
         load_w(1, 1, 0)
         load_w(1, 1, 1)
         load_w2(1)
-        nc.sync.dma_start(gate_sb[:], gate)
+        load_gate(1)
         nc.sync.dma_start(xr_sb[:], xr)
 
-        def cast(dst, src, cut):
+        staged = {}
+
+        def cast_x(s, half, first, tag, cut):
+            staged[s, half] = keep.tile([P, HALF * PACK], BF16, name="x_bf", tag=tag, align_bytes=64)
+            lo = (half * HALF - first) // 4
+            src = x_raw[s, first][:].rearrange("p t (c i) -> p c t i", i=4)[:, lo : lo + HALF // 4]
+            dst = staged[s, half][:].rearrange("p (c i t) -> p c t i", i=4, t=PACK)
             if cut > 0:
                 nc.scalar.activation(dst[:, :cut], src[:, :cut], COPY)
-            if cut < dst.shape[1]:
+            if cut < P:
                 nc.vector.tensor_copy(dst[:, cut:], src[:, cut:])
 
-        def cast_x(s, h, cut):
-            cols = slice(h * (HALF // 4), (h + 1) * (HALF // 4))
-            dst = x_bf[s][:].rearrange("p (c i t) -> p c t i", i=4, t=PACK)
-            src = x_raw[s][:].rearrange("p t (c i) -> p c t i", i=4)
-            cast(dst[:, cols], src[:, cols], cut)
+        def cast_w(key, tag, cut):
+            staged[key] = keep.tile([P, H * PACK], BF16, name="w_bf", tag=tag, align_bytes=64)
+            dst = staged[key][:].rearrange("p (t m j) -> p m j t", t=4, j=4)
+            src = w_raw[key][:].rearrange("p j (m t) -> p m j t", t=4)
+            nc.scalar.activation(dst[:, :cut], src[:, :cut], COPY)
+            if cut < P:
+                nc.vector.tensor_copy(dst[:, cut:], src[:, cut:])
 
-        def cast_w(e, g, s, cut, lo=0, hi=H // 4):
-            dst = w_bf[e, g, s][:].rearrange("p (t m j) -> p m j t", t=4, j=4)
-            src = w_raw[e, g, s][:].rearrange("p j (m t) -> p m j t", t=4)
-            cast(dst[:, lo:hi], src[:, lo:hi], cut)
+        def cast_w_last(key, tag):
+            staged[key] = keep.tile([P, H * PACK], BF16, name="w_bf", tag=tag, align_bytes=64)
+            dst = staged[key][:].rearrange("p (t m j) -> p m j t", t=4, j=4)
+            src = w_raw[key][:].rearrange("p j (m t) -> p m j t", t=4)
+            nc.scalar.activation(dst[:, :, :, :2], src[:, :, :, :2], COPY)
+            nc.vector.tensor_copy(dst[:, :, :, 2:], src[:, :, :, 2:])
 
-        def cast_w2(e, cut):
-            cast(
+        def cast_w2(e, tag):
+            w2_bf[e] = keep.tile([P, N, PACK], BF16, name=f"w2_bf{e}", tag=tag, align_bytes=64)
+            nc.scalar.activation(
                 w2_bf[e][:].rearrange("p (c i) t -> p c t i", i=4),
                 w2_raw[e][:].rearrange("p t (c i) -> p c t i", i=4),
-                cut,
+                COPY,
             )
 
-        def quant_x(s, h):
-            cols = slice(h * HALF, (h + 1) * HALF)
+        def quant_x(s, half):
+            cols = slice(half * HALF, (half + 1) * HALF)
             nc.vector.quantize_mx(
                 out=x_words[s][:, cols].bitcast(FP8X4),
                 scales=x_bytes[4 * s : P, cols],
-                in_=x_bf[s][:, h * HALF * PACK : (h + 1) * HALF * PACK],
+                in_=staged[s, half][:],
             )
 
-        def quant_w(e, g, s, lo=0, hi=H):
+        def quant_w(key, lo=0, hi=H):
             nc.vector.quantize_mx(
-                out=w_codes[e, g, s][:, lo:hi].bitcast(FP8X4),
-                scales=w_scales[e, g, s][:, lo:hi],
-                in_=w_bf[e, g, s][:, 4 * lo : 4 * hi],
+                out=w_codes[key][:, lo:hi].bitcast(FP8X4),
+                scales=w_scales[key][:, lo:hi],
+                in_=staged[key][:, PACK * lo : PACK * hi],
             )
 
         def quant_w2(e):
@@ -138,34 +149,41 @@ def tile_moe_res_glu_relu_kernel(tc, xT, xr, w1, w3, w2, gate, offs, out):
                 in_=w2_bf[e][:].rearrange("p w t -> p (w t)"),
             )
 
-        def product(e, g, b):
-            bank = psum.tile([P, 4, BLK], F32, name="bank")
-            cols = slice(e * C + b * BLK, e * C + (b + 1) * BLK)
-            for t in range(4):
-                for s in range(PASSES):
-                    nc.tensor.matmul_mx(
-                        out=bank[:, t, :],
-                        lhsT=w_codes[e, g, s][:, t * P : (t + 1) * P].bitcast(FP8X4),
-                        lhsT_scale=w_scales[e, g, s][:, t * P : (t + 1) * P],
-                        rhs=slot_words[s][:, cols].bitcast(FP8X4),
-                        rhs_scale=slot_bytes[4 * s : P, cols],
-                        start=(s == 0),
-                        stop=(s == PASSES - 1),
-                    )
-            return bank
+        def gather_words(s):
+            nc.vector.tensor_copy(slot_words[s][:], x_words[s][:].indirect(offsets[:]))
+
+        def gather_bytes():
+            nc.vector.tensor_copy(slot_bytes[:], x_bytes[:].indirect(offsets[:]))
 
         banks, relu_a, h_bf, y_banks = {}, {}, {}, {}
         h_codes = [keep.tile([P, C], U32, name=f"h_codes{e}", align_bytes=64) for e in range(E)]
         h_scales = [keep.tile([P, C], U8, name=f"h_scales{e}", align_bytes=64) for e in range(E)]
-        y_sb = [keep.tile([P, C], F32, name=f"y_sb{e}") for e in range(E)]
+        y_sb = {}
 
-        def products(e, g):
+        def products(e, g, t_groups=((0, 1, 2, 3),)):
             for b in range(2):
-                banks[e, g, b] = product(e, g, b)
+                banks[e, g, b] = psum.tile([P, 4, BLK], F32, name="bank")
+            for t_group in t_groups:
+                for b in range(2):
+                    cols = slice(e * C + b * BLK, e * C + (b + 1) * BLK)
+                    for t in t_group:
+                        for s in range(PASSES):
+                            nc.tensor.matmul_mx(
+                                out=banks[e, g, b][:, t, :],
+                                lhsT=w_codes[e, g, s][:, t * P : (t + 1) * P].bitcast(FP8X4),
+                                lhsT_scale=w_scales[e, g, s][:, t * P : (t + 1) * P],
+                                rhs=slot_words[s][:, cols].bitcast(FP8X4),
+                                rhs_scale=slot_bytes[4 * s : P, cols],
+                                start=(s == 0),
+                                stop=(s == PASSES - 1),
+                            )
 
-        def relu(e, b):
-            relu_a[e, b] = keep.tile([P, BLK, 4], F32, name=f"relu{e}{b}")
-            nc.scalar.activation(relu_a[e, b][:], banks[e, 0, b][:].rearrange("p t n -> p n t"), RELU)
+        def relu(e, b, tile):
+            relu_a[e, b] = tile.rearrange("p (n t) -> p n t", t=4)
+            nc.scalar.activation(relu_a[e, b], banks[e, 0, b][:].rearrange("p t n -> p n t"), RELU)
+
+        def scratch(width, tag):
+            return keep.tile([P, width], F32, name="scratch", tag=tag, align_bytes=64)
 
         def hmul(e, b):
             if b == 0:
@@ -173,21 +191,20 @@ def tile_moe_res_glu_relu_kernel(tc, xT, xr, w1, w3, w2, gate, offs, out):
             nc.vector.tensor_tensor(
                 h_bf[e][:, b * BLK : (b + 1) * BLK, :],
                 banks[e, 1, b][:].rearrange("p t n -> p n t"),
-                relu_a[e, b][:],
+                relu_a[e, b],
                 MULT,
             )
 
-        def down(e, b):
-            if b == 0:
-                y_banks[e] = psum_y.tile([P, C], F32, name="y_bank")
-            cols = slice(b * BLK, (b + 1) * BLK)
+        def down(e, lo, hi):
+            y_banks[e, lo] = psum.tile([P, hi - lo], F32, name="bank")
+            cols = slice(lo, hi)
             nc.vector.quantize_mx(
                 out=h_codes[e][:, cols].bitcast(FP8X4),
                 scales=h_scales[e][:, cols],
                 in_=h_bf[e][:, cols, :].rearrange("p n t -> p (n t)"),
             )
             nc.tensor.matmul_mx(
-                out=y_banks[e][:, cols],
+                out=y_banks[e, lo][:],
                 lhsT=w2_codes[e][:].bitcast(FP8X4),
                 lhsT_scale=w2_scales[e][:],
                 rhs=h_codes[e][:, cols].bitcast(FP8X4),
@@ -196,89 +213,79 @@ def tile_moe_res_glu_relu_kernel(tc, xT, xr, w1, w3, w2, gate, offs, out):
                 stop=True,
             )
 
-        def down_both(e):
-            y_banks[e] = psum_y.tile([P, C], F32, name="y_bank")
-            nc.vector.quantize_mx(
-                out=h_codes[e][:].bitcast(FP8X4),
-                scales=h_scales[e][:],
-                in_=h_bf[e][:].rearrange("p n t -> p (n t)"),
-            )
-            nc.tensor.matmul_mx(
-                out=y_banks[e][:],
-                lhsT=w2_codes[e][:].bitcast(FP8X4),
-                lhsT_scale=w2_scales[e][:],
-                rhs=h_codes[e][:].bitcast(FP8X4),
-                rhs_scale=h_scales[e][:],
-                start=True,
-                stop=True,
-            )
-
-        def ycopy(e, lo=0, hi=C):
-            nc.scalar.activation(y_sb[e][:, lo:hi], y_banks[e][:, lo:hi], COPY)
+        def ycopy(e, lo, hi, tile, first):
+            y_sb[e, lo] = tile
+            nc.scalar.activation(tile, y_banks[e, first][:, lo - first : hi - first], COPY)
 
         def scatter(e, lo, hi):
             first, last = e * C + lo, e * C + hi
             nc.vector.tensor_tensor(
                 window[:].indirect(offsets[:, first // 16 : last // 16]),
-                y_sb[e][:, lo:hi],
-                gate_sb[:, first:last],
+                y_sb[e, lo],
+                gate_sb[e][:, lo:hi],
                 MULT,
             )
 
-        cast_x(0, 1, 44)
+        def finish(lo, hi):
+            out_sb = keep.tile([P, hi - lo], F32, name=f"out_sb{lo}")
+            nc.vector.tensor_tensor(out_sb[:], window[:, lo:hi], xr_sb[:, lo:hi], ADD)
+            nc.sync.dma_start(out[:, lo:hi], out_sb[:])
+
+        cast_x(0, 0, 0, "x_bf00", 128)
+        cast_x(0, 1, 0, "x_bf01", 0)
         quant_x(0, 1)
-        cast_x(0, 0, 64)
         quant_x(0, 0)
-        nc.vector.tensor_copy(slot_words[0][:], x_words[0][:].indirect(offsets[:]))
-        cast_x(1, 1, 128)
-        cast_x(1, 0, 4)
+        gather_words(0)
+        cast_x(1, 0, 0, "x_bf10", 128)
         quant_x(1, 0)
-        cast_w(0, 0, 0, 100)
+        cast_x(1, 1, HALF, "x_words0", 64)
         quant_x(1, 1)
-        cast_w(0, 0, 1, 116)
-        nc.vector.tensor_copy(slot_words[1][:], x_words[1][:].indirect(offsets[:]))
-        nc.vector.tensor_copy(slot_bytes[:], x_bytes[:].indirect(offsets[:]))
-        quant_w(0, 0, 0)
-        cast_w(0, 1, 0, 128)
-        quant_w(0, 0, 1)
-        cast_w(0, 1, 1, 48)
-        quant_w(0, 1, 0)
-        quant_w(0, 1, 1)
+        gather_words(1)
+        cast_w((0, 0, 0), "ring0", 128)
+        gather_bytes()
+        quant_w((0, 0, 0))
+        cast_w((0, 0, 1), "ring1", 80)
+        quant_w((0, 0, 1))
         products(0, 0)
-        relu(0, 0)
+        cast_w((0, 1, 0), "ring0", 72)
+        quant_w((0, 1, 0))
+        relu(0, 0, scratch(4 * BLK, "w_raw010")[:])
+        cast_w((0, 1, 1), "ring1", 72)
+        quant_w((0, 1, 1))
         products(0, 1)
-        cast_w2(0, 0)
-        quant_w2(0)
-        relu(0, 1)
-        cast_w(1, 0, 0, 84)
-        quant_w(1, 0, 0)
+        relu(0, 1, scratch(4 * BLK, "w_raw011")[:])
+        cast_w((1, 0, 0), "ring1", 80)
         hmul(0, 0)
+        quant_w((1, 0, 0))
         hmul(0, 1)
-        cast_w(1, 0, 1, 88)
-        down_both(0)
-        cast_w(1, 1, 0, 28)
-        quant_w(1, 1, 0)
-        quant_w(1, 0, 1)
-        cast_w(1, 1, 1, 36)
+        cast_w2(0, "w_raw100")
+        cast_w((1, 0, 1), "ring1", 80)
+        quant_w2(0)
+        down(0, 0, C)
+        quant_w((1, 0, 1))
         products(1, 0)
-        quant_w(1, 1, 1)
-        products(1, 1)
-        ycopy(0)
-        relu(1, 0)
-        cast_w2(1, 0)
-        relu(1, 1)
-        scatter(0, 0, C)
+        ycopy(0, 0, BLK, scratch(BLK, "y00")[:], 0)
+        scatter(0, 0, BLK)
+        cast_w((1, 1, 0), "ring1", 72)
+        quant_w((1, 1, 0))
+        relu(1, 0, scratch(4 * BLK, "w_raw110")[:])
+        cast_w_last((1, 1, 1), "ring1")
+        quant_w((1, 1, 1), 2 * P, H)
+        quant_w((1, 1, 1), 0, 2 * P)
+        products(1, 1, ((2, 3), (0, 1)))
+        late = scratch(5 * BLK, "w_raw111")
+        ycopy(0, BLK, C, late[:, :BLK], 0)
+        relu(1, 1, late[:, BLK:])
+        scatter(0, BLK, C)
+        cast_w2(1, "ring1")
         hmul(1, 0)
         quant_w2(1)
-        down(1, 0)
         hmul(1, 1)
-        ycopy(1, 0, 128)
+        down(1, 0, BLK)
+        ycopy(1, 0, BLK, scratch(BLK, "y10")[:], 0)
+        down(1, BLK, C)
         scatter(1, 0, BLK)
-        down(1, 1)
-        ycopy(1, 128, 256)
+        ycopy(1, BLK, C, scratch(BLK, "y11")[:], BLK)
         scatter(1, BLK, C)
-        for q in range(2):
-            cols = slice(q * HALF, (q + 1) * HALF)
-            out_sb = keep.tile([P, HALF], F32, name=f"out_sb{q}")
-            nc.vector.tensor_tensor(out_sb[:], window[:, cols], xr_sb[:, cols], ADD)
-            nc.sync.dma_start(out[:, cols], out_sb[:])
+        finish(0, HALF)
+        finish(HALF, T)

@@ -76,8 +76,7 @@ def tile_moe_res_glu_relu_kernel(tc, xT, xr, w1, w3, w2, gate, offs, out):
 
         load_x(0, 0, T)
         nc.sync.dma_start(offsets[:], offs)
-        load_x(1, 0, HALF)
-        load_x(1, HALF, T)
+        load_x(1, 0, T)
         load_w(0, 0, 0)
         load_w(0, 0, 1)
         load_w(0, 1, 0)
@@ -85,24 +84,21 @@ def tile_moe_res_glu_relu_kernel(tc, xT, xr, w1, w3, w2, gate, offs, out):
         load_w(1, 0, 0)
         load_w2(0)
         load_w(1, 0, 1)
-        load_gate(0)
         load_w(1, 1, 0)
         load_w(1, 1, 1)
+        load_gate(0)
         load_w2(1)
         load_gate(1)
         nc.sync.dma_start(xr_sb[:], xr)
 
         staged = {}
 
-        def cast_x(s, half, first, tag, cut):
-            staged[s, half] = keep.tile([P, HALF * PACK], BF16, name="x_bf", tag=tag, align_bytes=64)
-            lo = (half * HALF - first) // 4
-            src = x_raw[s, first][:].rearrange("p t (c i) -> p c t i", i=4)[:, lo : lo + HALF // 4]
-            dst = staged[s, half][:].rearrange("p (c i t) -> p c t i", i=4, t=PACK)
-            if cut > 0:
-                nc.scalar.activation(dst[:, :cut], src[:, :cut], COPY)
-            if cut < P:
-                nc.vector.tensor_copy(dst[:, cut:], src[:, cut:])
+        def cast_x(s, tag, cut):
+            staged[s] = keep.tile([P, T * PACK], BF16, name="x_bf", tag=tag, align_bytes=64)
+            src = x_raw[s, 0][:].rearrange("p t (c i) -> p c t i", i=4)
+            dst = staged[s][:].rearrange("p (c i t) -> p c t i", i=4, t=PACK)
+            nc.scalar.activation(dst[:, :cut], src[:, :cut], COPY)
+            nc.vector.tensor_copy(dst[:, cut:], src[:, cut:])
 
         def cast_w(key, tag, cut):
             staged[key] = keep.tile([P, H * PACK], BF16, name="w_bf", tag=tag, align_bytes=64)
@@ -132,7 +128,7 @@ def tile_moe_res_glu_relu_kernel(tc, xT, xr, w1, w3, w2, gate, offs, out):
             nc.vector.quantize_mx(
                 out=x_words[s][:, cols].bitcast(FP8X4),
                 scales=x_bytes[4 * s : P, cols],
-                in_=staged[s, half][:],
+                in_=staged[s][:, half * HALF * PACK : (half + 1) * HALF * PACK],
             )
 
         def quant_w(key, lo=0, hi=H):
@@ -195,20 +191,21 @@ def tile_moe_res_glu_relu_kernel(tc, xT, xr, w1, w3, w2, gate, offs, out):
                 MULT,
             )
 
+        def quant_h(e, lo, hi):
+            nc.vector.quantize_mx(
+                out=h_codes[e][:, lo:hi].bitcast(FP8X4),
+                scales=h_scales[e][:, lo:hi],
+                in_=h_bf[e][:, lo:hi, :].rearrange("p n t -> p (n t)"),
+            )
+
         def down(e, lo, hi):
             y_banks[e, lo] = psum.tile([P, hi - lo], F32, name="bank")
-            cols = slice(lo, hi)
-            nc.vector.quantize_mx(
-                out=h_codes[e][:, cols].bitcast(FP8X4),
-                scales=h_scales[e][:, cols],
-                in_=h_bf[e][:, cols, :].rearrange("p n t -> p (n t)"),
-            )
             nc.tensor.matmul_mx(
                 out=y_banks[e, lo][:],
                 lhsT=w2_codes[e][:].bitcast(FP8X4),
                 lhsT_scale=w2_scales[e][:],
-                rhs=h_codes[e][:, cols].bitcast(FP8X4),
-                rhs_scale=h_scales[e][:, cols],
+                rhs=h_codes[e][:, lo:hi].bitcast(FP8X4),
+                rhs_scale=h_scales[e][:, lo:hi],
                 start=True,
                 stop=True,
             )
@@ -231,58 +228,57 @@ def tile_moe_res_glu_relu_kernel(tc, xT, xr, w1, w3, w2, gate, offs, out):
             nc.vector.tensor_tensor(out_sb[:], window[:, lo:hi], xr_sb[:, lo:hi], ADD)
             nc.sync.dma_start(out[:, lo:hi], out_sb[:])
 
-        cast_x(0, 0, 0, "x_bf00", 128)
-        cast_x(0, 1, 0, "x_bf01", 0)
+        cast_x(0, "x_bf0", 112)
         quant_x(0, 1)
         quant_x(0, 0)
         gather_words(0)
-        cast_x(1, 0, 0, "x_bf10", 128)
-        quant_x(1, 0)
-        cast_x(1, 1, HALF, "x_words0", 64)
+        cast_x(1, "x_words0", 112)
         quant_x(1, 1)
+        quant_x(1, 0)
         gather_words(1)
         cast_w((0, 0, 0), "ring0", 128)
         gather_bytes()
         quant_w((0, 0, 0))
-        cast_w((0, 0, 1), "ring1", 80)
+        cast_w((0, 0, 1), "ring1", 64)
         quant_w((0, 0, 1))
         products(0, 0)
-        cast_w((0, 1, 0), "ring0", 72)
+        cast_w((0, 1, 0), "ring0", 64)
         quant_w((0, 1, 0))
-        relu(0, 0, scratch(4 * BLK, "w_raw010")[:])
-        cast_w((0, 1, 1), "ring1", 72)
+        cast_w((0, 1, 1), "ring1", 56)
         quant_w((0, 1, 1))
         products(0, 1)
-        relu(0, 1, scratch(4 * BLK, "w_raw011")[:])
-        cast_w((1, 0, 0), "ring1", 80)
+        relu(0, 0, scratch(4 * BLK, "w_raw011")[:])
+        cast_w((1, 0, 0), "ring1", 56)
         hmul(0, 0)
         quant_w((1, 0, 0))
+        relu(0, 1, scratch(4 * BLK, "w_raw100")[:])
+        cast_w2(0, "w_raw011")
         hmul(0, 1)
-        cast_w2(0, "w_raw100")
-        cast_w((1, 0, 1), "ring1", 80)
+        cast_w((1, 0, 1), "ring1", 56)
         quant_w2(0)
-        down(0, 0, C)
+        quant_h(0, 0, C)
         quant_w((1, 0, 1))
+        down(0, 0, C)
         products(1, 0)
-        ycopy(0, 0, BLK, scratch(BLK, "y00")[:], 0)
-        scatter(0, 0, BLK)
-        cast_w((1, 1, 0), "ring1", 72)
+        cast_w((1, 1, 0), "ring1", 48)
         quant_w((1, 1, 0))
         relu(1, 0, scratch(4 * BLK, "w_raw110")[:])
         cast_w_last((1, 1, 1), "ring1")
         quant_w((1, 1, 1), 2 * P, H)
         quant_w((1, 1, 1), 0, 2 * P)
         products(1, 1, ((2, 3), (0, 1)))
-        late = scratch(5 * BLK, "w_raw111")
-        ycopy(0, BLK, C, late[:, :BLK], 0)
-        relu(1, 1, late[:, BLK:])
-        scatter(0, BLK, C)
+        late = scratch(C + 4 * BLK, "w_raw111")
+        ycopy(0, 0, C, late[:, :C], 0)
+        scatter(0, 0, C)
+        relu(1, 1, late[:, C:])
         cast_w2(1, "ring1")
         hmul(1, 0)
         quant_w2(1)
-        hmul(1, 1)
+        quant_h(1, 0, BLK)
         down(1, 0, BLK)
+        hmul(1, 1)
         ycopy(1, 0, BLK, scratch(BLK, "y10")[:], 0)
+        quant_h(1, BLK, C)
         down(1, BLK, C)
         scatter(1, 0, BLK)
         ycopy(1, BLK, C, scratch(BLK, "y11")[:], BLK)

@@ -108,13 +108,6 @@ def tile_moe_res_glu_relu_kernel(tc, xT, xr, w1, w3, w2, gate, offs, out):
             if cut < P:
                 nc.vector.tensor_copy(dst[:, cut:], src[:, cut:])
 
-        def cast_w_last(key, tag):
-            staged[key] = keep.tile([P, H * PACK], BF16, name="w_bf", tag=tag, align_bytes=64)
-            dst = staged[key][:].rearrange("p (t m j) -> p m j t", t=4, j=4)
-            src = w_raw[key][:].rearrange("p j (m t) -> p m j t", t=4)
-            nc.scalar.activation(dst[:, :, :, :2], src[:, :, :, :2], COPY)
-            nc.vector.tensor_copy(dst[:, :, :, 2:], src[:, :, :, 2:])
-
         def cast_w2(e, tag):
             w2_bf[e] = keep.tile([P, N, PACK], BF16, name=f"w2_bf{e}", tag=tag, align_bytes=64)
             nc.scalar.activation(
@@ -151,10 +144,12 @@ def tile_moe_res_glu_relu_kernel(tc, xT, xr, w1, w3, w2, gate, offs, out):
         def gather_bytes():
             nc.vector.tensor_copy(slot_bytes[:], x_bytes[:].indirect(offsets[:]))
 
-        banks, relu_a, h_bf, y_banks = {}, {}, {}, {}
+        banks, relu_a, y_banks = {}, {}, {}
         h_codes = [keep.tile([P, C], U32, name=f"h_codes{e}", align_bytes=64) for e in range(E)]
         h_scales = [keep.tile([P, C], U8, name=f"h_scales{e}", align_bytes=64) for e in range(E)]
         y_sb = {}
+        h_first = keep.tile([P, C * PACK], BF16, name="h_first", align_bytes=64)
+        h_last = keep.tile([P, BLK * PACK], BF16, name="h_last", align_bytes=64)
 
         def products(e, g, t_groups=((0, 1, 2, 3),)):
             for b in range(2):
@@ -175,28 +170,25 @@ def tile_moe_res_glu_relu_kernel(tc, xT, xr, w1, w3, w2, gate, offs, out):
                             )
 
         def relu(e, b, tile):
-            relu_a[e, b] = tile.rearrange("p (n t) -> p n t", t=4)
-            nc.scalar.activation(relu_a[e, b], banks[e, 0, b][:].rearrange("p t n -> p n t"), RELU)
+            relu_a[e, b] = tile
+            nc.scalar.activation(tile, banks[e, 0, b][:].rearrange("p t (j n) -> p j n t", j=4), RELU)
+
+        def spent(key):
+            return w_raw[key][:, :, :BLK].rearrange("p j (n t) -> p j n t", t=4)
 
         def scratch(width, tag):
             return keep.tile([P, width], F32, name="scratch", tag=tag, align_bytes=64)
 
-        def hmul(e, b):
-            if b == 0:
-                h_bf[e] = keep.tile([P, C, 4], BF16, name=f"h_bf{e}", align_bytes=64)
+        def hmul(e, b, tile):
             nc.vector.tensor_tensor(
-                h_bf[e][:, b * BLK : (b + 1) * BLK, :],
-                banks[e, 1, b][:].rearrange("p t n -> p n t"),
+                tile.rearrange("p (j n t) -> p j n t", j=4, t=4),
+                banks[e, 1, b][:].rearrange("p t (j n) -> p j n t", j=4),
                 relu_a[e, b],
                 MULT,
             )
 
-        def quant_h(e, lo, hi):
-            nc.vector.quantize_mx(
-                out=h_codes[e][:, lo:hi].bitcast(FP8X4),
-                scales=h_scales[e][:, lo:hi],
-                in_=h_bf[e][:, lo:hi, :].rearrange("p n t -> p (n t)"),
-            )
+        def quant_h(e, lo, hi, tile):
+            nc.vector.quantize_mx(out=h_codes[e][:, lo:hi].bitcast(FP8X4), scales=h_scales[e][:, lo:hi], in_=tile)
 
         def down(e, lo, hi):
             y_banks[e, lo] = psum.tile([P, hi - lo], F32, name="bank")
@@ -232,53 +224,52 @@ def tile_moe_res_glu_relu_kernel(tc, xT, xr, w1, w3, w2, gate, offs, out):
         quant_x(0, 1)
         quant_x(0, 0)
         gather_words(0)
-        cast_x(1, "x_words0", 112)
+        cast_x(1, "x_bf1", 112)
         quant_x(1, 1)
         quant_x(1, 0)
         gather_words(1)
-        cast_w((0, 0, 0), "ring0", 128)
+        cast_w((0, 0, 0), "w_bf000", 128)
         gather_bytes()
+        cast_w((0, 0, 1), "w_bf001", 64)
         quant_w((0, 0, 0))
-        cast_w((0, 0, 1), "ring1", 64)
         quant_w((0, 0, 1))
         products(0, 0)
-        cast_w((0, 1, 0), "ring0", 64)
+        cast_w((0, 1, 0), "w_bf010", 64)
         quant_w((0, 1, 0))
-        cast_w((0, 1, 1), "ring1", 56)
+        cast_w((0, 1, 1), "w_bf011", 56)
         quant_w((0, 1, 1))
         products(0, 1)
-        relu(0, 0, scratch(4 * BLK, "w_raw011")[:])
-        cast_w((1, 0, 0), "ring1", 56)
-        hmul(0, 0)
+        relu(0, 0, spent((0, 1, 1)))
+        cast_w((1, 0, 0), "w_bf100", 40)
         quant_w((1, 0, 0))
-        relu(0, 1, scratch(4 * BLK, "w_raw100")[:])
-        cast_w2(0, "w_raw011")
-        hmul(0, 1)
-        cast_w((1, 0, 1), "ring1", 56)
+        hmul(0, 0, h_first[:, : BLK * PACK])
+        relu(0, 1, spent((1, 0, 0)))
+        cast_w2(0, "w2_bf0")
+        hmul(0, 1, h_first[:, BLK * PACK :])
+        cast_w((1, 0, 1), "w_bf101", 56)
         quant_w2(0)
-        quant_h(0, 0, C)
+        quant_h(0, 0, C, h_first[:])
         quant_w((1, 0, 1))
         down(0, 0, C)
         products(1, 0)
-        cast_w((1, 1, 0), "ring1", 48)
+        cast_w((1, 1, 0), "w_bf110", 56)
         quant_w((1, 1, 0))
-        relu(1, 0, scratch(4 * BLK, "w_raw110")[:])
-        cast_w_last((1, 1, 1), "ring1")
-        quant_w((1, 1, 1), 2 * P, H)
-        quant_w((1, 1, 1), 0, 2 * P)
-        products(1, 1, ((2, 3), (0, 1)))
-        late = scratch(C + 4 * BLK, "w_raw111")
+        cast_w((1, 1, 1), "w_bf111", 40)
+        quant_w((1, 1, 1))
+        products(1, 1)
+        late = scratch(C + 8 * BLK, "w_raw111")
         ycopy(0, 0, C, late[:, :C], 0)
         scatter(0, 0, C)
-        relu(1, 1, late[:, C:])
-        cast_w2(1, "ring1")
-        hmul(1, 0)
+        relu(1, 0, late[:, C : C + 4 * BLK].rearrange("p (j n t) -> p j n t", j=4, t=4))
+        relu(1, 1, late[:, C + 4 * BLK :].rearrange("p (j n t) -> p j n t", j=4, t=4))
+        cast_w2(1, "w2_bf1")
+        hmul(1, 0, h_last[:])
         quant_w2(1)
-        quant_h(1, 0, BLK)
+        quant_h(1, 0, BLK, h_last[:])
         down(1, 0, BLK)
-        hmul(1, 1)
+        hmul(1, 1, h_last[:])
         ycopy(1, 0, BLK, scratch(BLK, "y10")[:], 0)
-        quant_h(1, BLK, C)
+        quant_h(1, BLK, C, h_last[:])
         down(1, BLK, C)
         scatter(1, 0, BLK)
         ycopy(1, BLK, C, scratch(BLK, "y11")[:], BLK)

@@ -11,7 +11,14 @@ PACK = 4
 K_PASS = P * PACK
 PASSES = K // K_PASS
 BLK = 128
+BLOCKS = C // BLK
 HALF = T // 2
+W1, W3 = 0, 1
+FIRST, LAST = 0, 1
+
+X_SHARE = 112
+W_SHARE = 64
+W_SHARE_URGENT = 40
 
 F32 = mybir.dt.float32
 BF16 = mybir.dt.bfloat16
@@ -31,169 +38,124 @@ def tile_moe_res_glu_relu_kernel(tc, xT, xr, w1, w3, w2, gate, offs, out):
         keep = ctx.enter_context(tc.tile_pool(name="keep", bufs=1))
         psum = ctx.enter_context(tc.psum_pool(name="psum", bufs=8))
 
-        offsets = keep.tile([P, S // 16], U16, name="offsets")
+        def sbuf(name, shape, dtype):
+            return keep.tile(shape, dtype, name=name, tag=name, align_bytes=64)
 
-        x_raw = {}
-        x_words = [keep.tile([P, T], U32, name=f"x_words{s}", tag=f"x_words{s}", align_bytes=64) for s in range(PASSES)]
-        x_bytes = keep.tile([P, T], U8, name="x_bytes", align_bytes=64)
-        slot_words = [keep.tile([P, S], U32, name=f"slot_words{s}", align_bytes=64) for s in range(PASSES)]
-        slot_bytes = keep.tile([P, S], U8, name="slot_bytes", align_bytes=64)
-        window = keep.tile([P, T], F32, name="window")
+        chunks = [(e, g, s) for e in range(E) for g in (W1, W3) for s in range(PASSES)]
+
+        offsets = keep.tile([P, S // 16], U16, name="offsets")
+        x_raw = [sbuf(f"x_raw{s}", [P, PACK, T], F32) for s in range(PASSES)]
+        x_bf = [sbuf(f"x_bf{s}", [P, T * PACK], BF16) for s in range(PASSES)]
+        x_words = [sbuf(f"x_words{s}", [P, T], U32) for s in range(PASSES)]
+        x_bytes = sbuf("x_bytes", [P, T], U8)
+        slot_words = [sbuf(f"slot_words{s}", [P, S], U32) for s in range(PASSES)]
+        slot_bytes = sbuf("slot_bytes", [P, S], U8)
+        w_raw = {c: sbuf("w_raw%d%d%d" % c, [P, PACK, H], F32) for c in chunks}
+        w_bf = {c: sbuf("w_bf%d%d%d" % c, [P, H * PACK], BF16) for c in chunks}
+        w_codes = {c: sbuf("w_codes%d%d%d" % c, [P, H], U32) for c in chunks}
+        w_scales = {c: sbuf("w_scales%d%d%d" % c, [P, H], U8) for c in chunks}
+        w2_raw = [sbuf(f"w2_raw{e}", [P, PACK, N], F32) for e in range(E)]
+        w2_bf = [sbuf(f"w2_bf{e}", [P, N * PACK], BF16) for e in range(E)]
+        w2_codes = [sbuf(f"w2_codes{e}", [P, N], U32) for e in range(E)]
+        w2_scales = [sbuf(f"w2_scales{e}", [P, N], U8) for e in range(E)]
+        h_codes = [sbuf(f"h_codes{e}", [P, C], U32) for e in range(E)]
+        h_scales = [sbuf(f"h_scales{e}", [P, C], U8) for e in range(E)]
+        gate_sb = [sbuf(f"gate{e}", [P, C], F32) for e in range(E)]
+        xr_sb = sbuf("xr", [P, T], F32)
+        window = sbuf("window", [P, T], F32)
+
         nc.gpsimd.memset(x_bytes[:], 0)
         nc.gpsimd.memset(window[:], 0.0)
 
-        w_raw, w_codes, w_scales = {}, {}, {}
-        for e in range(E):
-            for g in range(2):
-                for s in range(PASSES):
-                    key = (e, g, s)
-                    w_raw[key] = keep.tile([P, PACK, H], F32, name=f"w_raw{e}{g}{s}", tag=f"w_raw{e}{g}{s}", align_bytes=64)
-                    w_codes[key] = keep.tile([P, H], U32, name=f"w_codes{e}{g}{s}", align_bytes=64)
-                    w_scales[key] = keep.tile([P, H], U8, name=f"w_scales{e}{g}{s}", align_bytes=64)
-        w2_raw = [keep.tile([P, PACK, N], F32, name=f"w2_raw{e}") for e in range(E)]
-        w2_bf = {}
-        w2_codes = [keep.tile([P, N], U32, name=f"w2_codes{e}", align_bytes=64) for e in range(E)]
-        w2_scales = [keep.tile([P, N], U8, name=f"w2_scales{e}", align_bytes=64) for e in range(E)]
-        gate_sb = [keep.tile([P, C], F32, name=f"gate_sb{e}") for e in range(E)]
-        xr_sb = keep.tile([P, T], F32, name="xr_sb")
+        def load_rows(tile, rows):
+            nc.sync.dma_start(tile[:], rows.rearrange("(p j) w -> p j w", j=PACK))
 
-        weights = (w1, w3)
+        def load_chunk(e, g, s):
+            load_rows(w_raw[e, g, s], (w1, w3)[g][e][s * K_PASS : (s + 1) * K_PASS, :])
 
-        def load_x(s, lo, hi):
-            x_raw[s, lo] = keep.tile([P, PACK, hi - lo], F32, name=f"x_raw{s}_{lo}")
-            rows = xT[s * K_PASS : (s + 1) * K_PASS, lo:hi]
-            nc.sync.dma_start(x_raw[s, lo][:], rows.rearrange("(p j) w -> p j w", j=PACK))
-
-        def load_w(e, g, s):
-            rows = weights[g][e][s * K_PASS : (s + 1) * K_PASS, :]
-            nc.sync.dma_start(w_raw[e, g, s][:], rows.rearrange("(p j) w -> p j w", j=PACK))
-
-        def load_w2(e):
-            nc.sync.dma_start(w2_raw[e][:], w2[e].rearrange("(p j) n -> p j n", j=PACK))
-
-        def load_gate(e):
-            nc.sync.dma_start(gate_sb[e][:], gate[:, e * C : (e + 1) * C])
-
-        load_x(0, 0, T)
+        load_rows(x_raw[0], xT[:K_PASS, :])
         nc.sync.dma_start(offsets[:], offs)
-        load_x(1, 0, T)
-        load_w(0, 0, 0)
-        load_w(0, 0, 1)
-        load_w(0, 1, 0)
-        load_w(0, 1, 1)
-        load_w(1, 0, 0)
-        load_w2(0)
-        load_w(1, 0, 1)
-        load_w(1, 1, 0)
-        load_w(1, 1, 1)
-        load_gate(0)
-        load_w2(1)
-        load_gate(1)
+        load_rows(x_raw[1], xT[K_PASS:, :])
+        for c in chunks:
+            load_chunk(*c)
+            if c == (LAST, W1, 0):
+                load_rows(w2_raw[FIRST], w2[FIRST])
+        nc.sync.dma_start(gate_sb[FIRST][:], gate[:, :C])
+        load_rows(w2_raw[LAST], w2[LAST])
+        nc.sync.dma_start(gate_sb[LAST][:], gate[:, C:])
         nc.sync.dma_start(xr_sb[:], xr)
 
-        staged = {}
+        def cast(dst, src, share):
+            nc.scalar.activation(dst[:, :share], src[:, :share], COPY)
+            if share < dst.shape[1]:
+                nc.vector.tensor_copy(dst[:, share:], src[:, share:])
 
-        def cast_x(s, tag, cut):
-            staged[s] = keep.tile([P, T * PACK], BF16, name="x_bf", tag=tag, align_bytes=64)
-            src = x_raw[s, 0][:].rearrange("p t (c i) -> p c t i", i=4)
-            dst = staged[s][:].rearrange("p (c i t) -> p c t i", i=4, t=PACK)
-            nc.scalar.activation(dst[:, :cut], src[:, :cut], COPY)
-            nc.vector.tensor_copy(dst[:, cut:], src[:, cut:])
-
-        def cast_w(key, tag, cut):
-            staged[key] = keep.tile([P, H * PACK], BF16, name="w_bf", tag=tag, align_bytes=64)
-            dst = staged[key][:].rearrange("p (t m j) -> p m j t", t=4, j=4)
-            src = w_raw[key][:].rearrange("p j (m t) -> p m j t", t=4)
-            nc.scalar.activation(dst[:, :cut], src[:, :cut], COPY)
-            if cut < P:
-                nc.vector.tensor_copy(dst[:, cut:], src[:, cut:])
-
-        def cast_w2(e, tag):
-            w2_bf[e] = keep.tile([P, N, PACK], BF16, name=f"w2_bf{e}", tag=tag, align_bytes=64)
-            nc.scalar.activation(
-                w2_bf[e][:].rearrange("p (c i) t -> p c t i", i=4),
-                w2_raw[e][:].rearrange("p t (c i) -> p c t i", i=4),
-                COPY,
+        def cast_rows(bf, raw, share):
+            cast(
+                bf[:].rearrange("p (c i j) -> p c j i", i=4, j=PACK),
+                raw[:].rearrange("p j (c i) -> p c j i", i=4),
+                share,
             )
 
-        def quant_x(s, half):
-            cols = slice(half * HALF, (half + 1) * HALF)
-            nc.vector.quantize_mx(
-                out=x_words[s][:, cols].bitcast(FP8X4),
-                scales=x_bytes[4 * s : P, cols],
-                in_=staged[s][:, half * HALF * PACK : (half + 1) * HALF * PACK],
+        def cast_chunk(c, share):
+            cast(
+                w_bf[c][:].rearrange("p (t m j) -> p m j t", t=PACK, j=PACK),
+                w_raw[c][:].rearrange("p j (m t) -> p m j t", t=PACK),
+                share,
             )
 
-        def quant_w(key, lo=0, hi=H):
-            nc.vector.quantize_mx(
-                out=w_codes[key][:, lo:hi].bitcast(FP8X4),
-                scales=w_scales[key][:, lo:hi],
-                in_=staged[key][:, PACK * lo : PACK * hi],
-            )
+        def quantize(codes, scales, values):
+            nc.vector.quantize_mx(out=codes.bitcast(FP8X4), scales=scales, in_=values)
 
-        def quant_w2(e):
-            nc.vector.quantize_mx(
-                out=w2_codes[e][:].bitcast(FP8X4),
-                scales=w2_scales[e][:],
-                in_=w2_bf[e][:].rearrange("p w t -> p (w t)"),
-            )
+        def quantize_chunk(c):
+            quantize(w_codes[c][:], w_scales[c][:], w_bf[c][:])
 
-        def gather_words(s):
+        def tokens_to_slots(s):
+            cast_rows(x_bf[s], x_raw[s], X_SHARE)
+            for lo in (HALF, 0):
+                cols = slice(lo, lo + HALF)
+                quantize(x_words[s][:, cols], x_bytes[4 * s : P, cols], x_bf[s][:, lo * PACK : (lo + HALF) * PACK])
             nc.vector.tensor_copy(slot_words[s][:], x_words[s][:].indirect(offsets[:]))
 
-        def gather_bytes():
-            nc.vector.tensor_copy(slot_bytes[:], x_bytes[:].indirect(offsets[:]))
+        def first_layer(e, g):
+            banks = []
+            for b in range(BLOCKS):
+                bank = psum.tile([P, PACK, BLK], F32, name="bank")
+                slots = slice(e * C + b * BLK, e * C + (b + 1) * BLK)
+                for t in range(PACK):
+                    cols = slice(t * P, (t + 1) * P)
+                    for s in range(PASSES):
+                        nc.tensor.matmul_mx(
+                            out=bank[:, t, :],
+                            lhsT=w_codes[e, g, s][:, cols].bitcast(FP8X4),
+                            lhsT_scale=w_scales[e, g, s][:, cols],
+                            rhs=slot_words[s][:, slots].bitcast(FP8X4),
+                            rhs_scale=slot_bytes[4 * s : P, slots],
+                            start=(s == 0),
+                            stop=(s == PASSES - 1),
+                        )
+                banks.append(bank)
+            return banks
 
-        banks, relu_a, y_banks = {}, {}, {}
-        h_codes = [keep.tile([P, C], U32, name=f"h_codes{e}", align_bytes=64) for e in range(E)]
-        h_scales = [keep.tile([P, C], U8, name=f"h_scales{e}", align_bytes=64) for e in range(E)]
-        y_sb = {}
-        h_first = keep.tile([P, C * PACK], BF16, name="h_first", align_bytes=64)
-        h_last = keep.tile([P, BLK * PACK], BF16, name="h_last", align_bytes=64)
+        def by_slot(bank):
+            return bank[:].rearrange("p t (r n) -> p r n t", r=4)
 
-        def products(e, g, t_groups=((0, 1, 2, 3),)):
-            for b in range(2):
-                banks[e, g, b] = psum.tile([P, 4, BLK], F32, name="bank")
-            for t_group in t_groups:
-                for b in range(2):
-                    cols = slice(e * C + b * BLK, e * C + (b + 1) * BLK)
-                    for t in t_group:
-                        for s in range(PASSES):
-                            nc.tensor.matmul_mx(
-                                out=banks[e, g, b][:, t, :],
-                                lhsT=w_codes[e, g, s][:, t * P : (t + 1) * P].bitcast(FP8X4),
-                                lhsT_scale=w_scales[e, g, s][:, t * P : (t + 1) * P],
-                                rhs=slot_words[s][:, cols].bitcast(FP8X4),
-                                rhs_scale=slot_bytes[4 * s : P, cols],
-                                start=(s == 0),
-                                stop=(s == PASSES - 1),
-                            )
+        def in_runs(flat):
+            return flat.rearrange("p (r n t) -> p r n t", r=4, t=PACK)
 
-        def relu(e, b, tile):
-            relu_a[e, b] = tile
-            nc.scalar.activation(tile, banks[e, 0, b][:].rearrange("p t (j n) -> p j n t", j=4), RELU)
+        def cast_part(c):
+            return w_raw[c][:, :, :BLK].rearrange("p r (n t) -> p r n t", t=PACK)
 
-        def spent(key):
-            return w_raw[key][:, :, :BLK].rearrange("p j (n t) -> p j n t", t=4)
+        def relu(dst, bank):
+            nc.scalar.activation(dst, by_slot(bank), RELU)
 
-        def scratch(width, tag):
-            return keep.tile([P, width], F32, name="scratch", tag=tag, align_bytes=64)
+        def gated(h_bf, bank, relu_values):
+            nc.vector.tensor_tensor(in_runs(h_bf), by_slot(bank), relu_values, MULT)
 
-        def hmul(e, b, tile):
-            nc.vector.tensor_tensor(
-                tile.rearrange("p (j n t) -> p j n t", j=4, t=4),
-                banks[e, 1, b][:].rearrange("p t (j n) -> p j n t", j=4),
-                relu_a[e, b],
-                MULT,
-            )
-
-        def quant_h(e, lo, hi, tile):
-            nc.vector.quantize_mx(out=h_codes[e][:, lo:hi].bitcast(FP8X4), scales=h_scales[e][:, lo:hi], in_=tile)
-
-        def down(e, lo, hi):
-            y_banks[e, lo] = psum.tile([P, hi - lo], F32, name="bank")
+        def second_layer(e, lo, hi):
+            bank = psum.tile([P, hi - lo], F32, name="bank")
             nc.tensor.matmul_mx(
-                out=y_banks[e, lo][:],
+                out=bank[:],
                 lhsT=w2_codes[e][:].bitcast(FP8X4),
                 lhsT_scale=w2_scales[e][:],
                 rhs=h_codes[e][:, lo:hi].bitcast(FP8X4),
@@ -201,78 +163,69 @@ def tile_moe_res_glu_relu_kernel(tc, xT, xr, w1, w3, w2, gate, offs, out):
                 start=True,
                 stop=True,
             )
+            return bank
 
-        def ycopy(e, lo, hi, tile, first):
-            y_sb[e, lo] = tile
-            nc.scalar.activation(tile, y_banks[e, first][:, lo - first : hi - first], COPY)
+        def scatter(e, lo, hi, y):
+            entries = offsets[:, (e * C + lo) // 16 : (e * C + hi) // 16]
+            nc.vector.tensor_tensor(window[:].indirect(entries), y, gate_sb[e][:, lo:hi], MULT)
 
-        def scatter(e, lo, hi):
-            first, last = e * C + lo, e * C + hi
-            nc.vector.tensor_tensor(
-                window[:].indirect(offsets[:, first // 16 : last // 16]),
-                y_sb[e, lo],
-                gate_sb[e][:, lo:hi],
-                MULT,
-            )
+        tokens_to_slots(0)
+        tokens_to_slots(1)
+        cast_chunk((FIRST, W1, 0), P)
+        nc.vector.tensor_copy(slot_bytes[:], x_bytes[:].indirect(offsets[:]))
+        cast_chunk((FIRST, W1, 1), W_SHARE)
+        for s in range(PASSES):
+            quantize_chunk((FIRST, W1, s))
+        a_first = first_layer(FIRST, W1)
+        for s in range(PASSES):
+            cast_chunk((FIRST, W3, s), W_SHARE)
+            quantize_chunk((FIRST, W3, s))
+        b_first = first_layer(FIRST, W3)
 
-        def finish(lo, hi):
-            out_sb = keep.tile([P, hi - lo], F32, name=f"out_sb{lo}")
-            nc.vector.tensor_tensor(out_sb[:], window[:, lo:hi], xr_sb[:, lo:hi], ADD)
-            nc.sync.dma_start(out[:, lo:hi], out_sb[:])
+        h_first = sbuf("h_first", [P, C * PACK], BF16)
+        relu(cast_part((FIRST, W3, 1)), a_first[0])
+        cast_chunk((LAST, W1, 0), W_SHARE_URGENT)
+        quantize_chunk((LAST, W1, 0))
+        gated(h_first[:, : BLK * PACK], b_first[0], cast_part((FIRST, W3, 1)))
+        relu(cast_part((LAST, W1, 0)), a_first[1])
+        cast_rows(w2_bf[FIRST], w2_raw[FIRST], N // 4)
+        gated(h_first[:, BLK * PACK :], b_first[1], cast_part((LAST, W1, 0)))
+        cast_chunk((LAST, W1, 1), W_SHARE)
+        quantize(w2_codes[FIRST][:], w2_scales[FIRST][:], w2_bf[FIRST][:])
+        quantize(h_codes[FIRST][:], h_scales[FIRST][:], h_first[:])
+        quantize_chunk((LAST, W1, 1))
+        y_first = second_layer(FIRST, 0, C)
+        a_last = first_layer(LAST, W1)
+        cast_chunk((LAST, W3, 0), W_SHARE)
+        quantize_chunk((LAST, W3, 0))
+        cast_chunk((LAST, W3, 1), W_SHARE_URGENT)
+        quantize_chunk((LAST, W3, 1))
+        b_last = first_layer(LAST, W3)
 
-        cast_x(0, "x_bf0", 112)
-        quant_x(0, 1)
-        quant_x(0, 0)
-        gather_words(0)
-        cast_x(1, "x_bf1", 112)
-        quant_x(1, 1)
-        quant_x(1, 0)
-        gather_words(1)
-        cast_w((0, 0, 0), "w_bf000", 128)
-        gather_bytes()
-        cast_w((0, 0, 1), "w_bf001", 64)
-        quant_w((0, 0, 0))
-        quant_w((0, 0, 1))
-        products(0, 0)
-        cast_w((0, 1, 0), "w_bf010", 64)
-        quant_w((0, 1, 0))
-        cast_w((0, 1, 1), "w_bf011", 56)
-        quant_w((0, 1, 1))
-        products(0, 1)
-        relu(0, 0, spent((0, 1, 1)))
-        cast_w((1, 0, 0), "w_bf100", 40)
-        quant_w((1, 0, 0))
-        hmul(0, 0, h_first[:, : BLK * PACK])
-        relu(0, 1, spent((1, 0, 0)))
-        cast_w2(0, "w2_bf0")
-        hmul(0, 1, h_first[:, BLK * PACK :])
-        cast_w((1, 0, 1), "w_bf101", 56)
-        quant_w2(0)
-        quant_h(0, 0, C, h_first[:])
-        quant_w((1, 0, 1))
-        down(0, 0, C)
-        products(1, 0)
-        cast_w((1, 1, 0), "w_bf110", 56)
-        quant_w((1, 1, 0))
-        cast_w((1, 1, 1), "w_bf111", 40)
-        quant_w((1, 1, 1))
-        products(1, 1)
-        late = scratch(C + 8 * BLK, "w_raw111")
-        ycopy(0, 0, C, late[:, :C], 0)
-        scatter(0, 0, C)
-        relu(1, 0, late[:, C : C + 4 * BLK].rearrange("p (j n t) -> p j n t", j=4, t=4))
-        relu(1, 1, late[:, C + 4 * BLK :].rearrange("p (j n t) -> p j n t", j=4, t=4))
-        cast_w2(1, "w2_bf1")
-        hmul(1, 0, h_last[:])
-        quant_w2(1)
-        quant_h(1, 0, BLK, h_last[:])
-        down(1, 0, BLK)
-        hmul(1, 1, h_last[:])
-        ycopy(1, 0, BLK, scratch(BLK, "y10")[:], 0)
-        quant_h(1, BLK, C, h_last[:])
-        down(1, BLK, C)
-        scatter(1, 0, BLK)
-        ycopy(1, BLK, C, scratch(BLK, "y11")[:], BLK)
-        scatter(1, BLK, C)
-        finish(0, HALF)
-        finish(HALF, T)
+        late = sbuf("w_raw%d%d%d" % chunks[-1], [P, C + BLOCKS * BLK * PACK], F32)
+        relu_last = [late[:, C + b * BLK * PACK : C + (b + 1) * BLK * PACK] for b in range(BLOCKS)]
+        nc.scalar.activation(late[:, :C], y_first[:], COPY)
+        scatter(FIRST, 0, C, late[:, :C])
+        for b in range(BLOCKS):
+            relu(in_runs(relu_last[b]), a_last[b])
+        cast_rows(w2_bf[LAST], w2_raw[LAST], N // 4)
+
+        h_last = [sbuf("h_last", [P, BLK * PACK], BF16)[:], w2_bf[LAST][:]]
+        y_last = [relu_last[1][:, :BLK], sbuf("y_last", [P, BLK], F32)[:]]
+        gated(h_last[0], b_last[0], in_runs(relu_last[0]))
+        quantize(w2_codes[LAST][:], w2_scales[LAST][:], w2_bf[LAST][:])
+        quantize(h_codes[LAST][:, :BLK], h_scales[LAST][:, :BLK], h_last[0])
+        y_bank = second_layer(LAST, 0, BLK)
+        gated(h_last[1], b_last[1], in_runs(relu_last[1]))
+        nc.scalar.activation(y_last[0], y_bank[:], COPY)
+        quantize(h_codes[LAST][:, BLK:], h_scales[LAST][:, BLK:], h_last[1])
+        y_bank = second_layer(LAST, BLK, C)
+        scatter(LAST, 0, BLK, y_last[0])
+        nc.scalar.activation(y_last[1], y_bank[:], COPY)
+        scatter(LAST, BLK, C, y_last[1])
+
+        for lo in (0, HALF):
+            cols = slice(lo, lo + HALF)
+            out_sb = sbuf(f"out{lo}", [P, HALF], F32)
+            nc.vector.tensor_tensor(out_sb[:], window[:, cols], xr_sb[:, cols], ADD)
+            nc.sync.dma_start(out[:, cols], out_sb[:])

@@ -17,8 +17,11 @@ W1, W3 = 0, 1
 FIRST, LAST = 0, 1
 
 X_SHARE = 112
-W_SHARE = 64
+W_SHARE = 56
 W_SHARE_URGENT = 40
+
+GATE_PARTS = ((FIRST, 0, BLK), (FIRST, BLK, C), (LAST, 0, C))
+WARM_UPS = 2
 
 F32 = mybir.dt.float32
 BF16 = mybir.dt.bfloat16
@@ -60,7 +63,7 @@ def tile_moe_res_glu_relu_kernel(tc, xT, xr, w1, w3, w2, gate, offs, out):
         w2_scales = [sbuf(f"w2_scales{e}", [P, N], U8) for e in range(E)]
         h_codes = [sbuf(f"h_codes{e}", [P, C], U32) for e in range(E)]
         h_scales = [sbuf(f"h_scales{e}", [P, C], U8) for e in range(E)]
-        gate_sb = [sbuf(f"gate{e}", [P, C], F32) for e in range(E)]
+        gate_sb = {(e, lo): sbuf(f"gate{e}_{lo}", [P, hi - lo], F32) for e, lo, hi in GATE_PARTS}
         xr_sb = sbuf("xr", [P, T], F32)
         window = sbuf("window", [P, T], F32)
 
@@ -80,9 +83,11 @@ def tile_moe_res_glu_relu_kernel(tc, xT, xr, w1, w3, w2, gate, offs, out):
             load_chunk(*c)
             if c == (LAST, W1, 0):
                 load_rows(w2_raw[FIRST], w2[FIRST])
-        nc.sync.dma_start(gate_sb[FIRST][:], gate[:, :C])
+            if c == (LAST, W3, 0):
+                nc.sync.dma_start(gate_sb[FIRST, 0][:], gate[:, :BLK])
+        nc.sync.dma_start(gate_sb[FIRST, BLK][:], gate[:, BLK:C])
         load_rows(w2_raw[LAST], w2[LAST])
-        nc.sync.dma_start(gate_sb[LAST][:], gate[:, C:])
+        nc.sync.dma_start(gate_sb[LAST, 0][:], gate[:, C:])
         nc.sync.dma_start(xr_sb[:], xr)
 
         def cast(dst, src, share):
@@ -165,9 +170,9 @@ def tile_moe_res_glu_relu_kernel(tc, xT, xr, w1, w3, w2, gate, offs, out):
             )
             return bank
 
-        def scatter(e, lo, hi, y):
+        def scatter(e, lo, hi, y, gates):
             entries = offsets[:, (e * C + lo) // 16 : (e * C + hi) // 16]
-            nc.vector.tensor_tensor(window[:].indirect(entries), y, gate_sb[e][:, lo:hi], MULT)
+            nc.vector.tensor_tensor(window[:].indirect(entries), y, gates, MULT)
 
         tokens_to_slots(0)
         tokens_to_slots(1)
@@ -196,16 +201,30 @@ def tile_moe_res_glu_relu_kernel(tc, xT, xr, w1, w3, w2, gate, offs, out):
         quantize_chunk((LAST, W1, 1))
         y_first = second_layer(FIRST, 0, C)
         a_last = first_layer(LAST, W1)
+        y_early = sbuf("y_early", [P, BLK], F32)
+        nc.scalar.activation(y_early[:], y_first[:, :BLK], COPY)
         cast_chunk((LAST, W3, 0), W_SHARE)
+        scatter(FIRST, 0, BLK, y_early[:], gate_sb[FIRST, 0][:])
         quantize_chunk((LAST, W3, 0))
+        warm = psum.tile([P, S], F32, name="bank")
+        for u in range(WARM_UPS):
+            nc.tensor.matmul_mx(
+                out=warm[:],
+                lhsT=w_codes[LAST, W3, 0][:, :P].bitcast(FP8X4),
+                lhsT_scale=w_scales[LAST, W3, 0][:, :P],
+                rhs=slot_words[0][:].bitcast(FP8X4),
+                rhs_scale=slot_bytes[:],
+                start=True,
+                stop=True,
+            )
         cast_chunk((LAST, W3, 1), W_SHARE_URGENT)
         quantize_chunk((LAST, W3, 1))
         b_last = first_layer(LAST, W3)
 
         late = sbuf("w_raw%d%d%d" % chunks[-1], [P, C + BLOCKS * BLK * PACK], F32)
         relu_last = [late[:, C + b * BLK * PACK : C + (b + 1) * BLK * PACK] for b in range(BLOCKS)]
-        nc.scalar.activation(late[:, :C], y_first[:], COPY)
-        scatter(FIRST, 0, C, late[:, :C])
+        nc.scalar.activation(late[:, :BLK], y_first[:, BLK:], COPY)
+        scatter(FIRST, BLK, C, late[:, :BLK], gate_sb[FIRST, BLK][:])
         for b in range(BLOCKS):
             relu(in_runs(relu_last[b]), a_last[b])
         cast_rows(w2_bf[LAST], w2_raw[LAST], N // 4)
@@ -220,9 +239,9 @@ def tile_moe_res_glu_relu_kernel(tc, xT, xr, w1, w3, w2, gate, offs, out):
         nc.scalar.activation(y_last[0], y_bank[:], COPY)
         quantize(h_codes[LAST][:, BLK:], h_scales[LAST][:, BLK:], h_last[1])
         y_bank = second_layer(LAST, BLK, C)
-        scatter(LAST, 0, BLK, y_last[0])
+        scatter(LAST, 0, BLK, y_last[0], gate_sb[LAST, 0][:, :BLK])
         nc.scalar.activation(y_last[1], y_bank[:], COPY)
-        scatter(LAST, BLK, C, y_last[1])
+        scatter(LAST, BLK, C, y_last[1], gate_sb[LAST, 0][:, BLK:])
 
         for lo in (0, HALF):
             cols = slice(lo, lo + HALF)

@@ -17,11 +17,14 @@ W1, W3 = 0, 1
 FIRST, LAST = 0, 1
 
 X_SHARE = 112
-W_SHARE = 56
+W_SHARE = 64
 W_SHARE_URGENT = 40
+W_SHARE_BUSY = 56
+END_SHARE = 96
 
+END = H * PACK // 2
+LAP = 32
 GATE_PARTS = ((FIRST, 0, BLK), (FIRST, BLK, C), (LAST, 0, C))
-WARM_UPS = 2
 
 F32 = mybir.dt.float32
 BF16 = mybir.dt.bfloat16
@@ -39,12 +42,16 @@ def tile_moe_res_glu_relu_kernel(tc, xT, xr, w1, w3, w2, gate, offs, out):
     nc = tc.nc
     with ExitStack() as ctx:
         keep = ctx.enter_context(tc.tile_pool(name="keep", bufs=1))
-        psum = ctx.enter_context(tc.psum_pool(name="psum", bufs=8))
+        psum = ctx.enter_context(tc.psum_pool(name="psum", bufs=1))
 
         def sbuf(name, shape, dtype):
             return keep.tile(shape, dtype, name=name, tag=name, align_bytes=64)
 
+        def bank_tile(number, shape):
+            return psum.tile(shape, F32, name=f"bank{number}", tag=f"bank{number}")
+
         chunks = [(e, g, s) for e in range(E) for g in (W1, W3) for s in range(PASSES)]
+        end = chunks[-1]
 
         offsets = keep.tile([P, S // 16], U16, name="offsets")
         x_raw = [sbuf(f"x_raw{s}", [P, PACK, T], F32) for s in range(PASSES)]
@@ -54,11 +61,17 @@ def tile_moe_res_glu_relu_kernel(tc, xT, xr, w1, w3, w2, gate, offs, out):
         slot_words = [sbuf(f"slot_words{s}", [P, S], U32) for s in range(PASSES)]
         slot_bytes = sbuf("slot_bytes", [P, S], U8)
         w_raw = {c: sbuf("w_raw%d%d%d" % c, [P, PACK, H], F32) for c in chunks}
-        w_bf = {c: sbuf("w_bf%d%d%d" % c, [P, H * PACK], BF16) for c in chunks}
+        w_bf = {c: sbuf("w_bf%d%d%d" % c, [P, H * PACK], BF16) for c in chunks[:-1]}
         w_codes = {c: sbuf("w_codes%d%d%d" % c, [P, H], U32) for c in chunks}
         w_scales = {c: sbuf("w_scales%d%d%d" % c, [P, H], U8) for c in chunks}
         w2_raw = [sbuf(f"w2_raw{e}", [P, PACK, N], F32) for e in range(E)]
-        w2_bf = [sbuf(f"w2_bf{e}", [P, N * PACK], BF16) for e in range(E)]
+        upper = sbuf("upper", [P, 2 * (BLK + BLK * PACK)], BF16)
+        lower = sbuf("lower", [P, N * PACK + 2 * BLK * PACK], BF16)
+        end_upper = upper[:, 2 * BLK - LAP : 2 * BLK - LAP + END]
+        end_lower = lower[:, N * PACK - LAP : N * PACK - LAP + END]
+        y_late = upper[:, : 2 * BLK].bitcast(F32)
+        relu_last = [upper[:, 2 * BLK :].bitcast(F32), lower[:, N * PACK :].bitcast(F32)]
+        w2_bf = [sbuf("w2_bf0", [P, N * PACK], BF16)[:], lower[:, : N * PACK]]
         w2_codes = [sbuf(f"w2_codes{e}", [P, N], U32) for e in range(E)]
         w2_scales = [sbuf(f"w2_scales{e}", [P, N], U8) for e in range(E)]
         h_codes = [sbuf(f"h_codes{e}", [P, C], U32) for e in range(E)]
@@ -97,7 +110,7 @@ def tile_moe_res_glu_relu_kernel(tc, xT, xr, w1, w3, w2, gate, offs, out):
 
         def cast_rows(bf, raw, share):
             cast(
-                bf[:].rearrange("p (c i j) -> p c j i", i=4, j=PACK),
+                bf.rearrange("p (c i j) -> p c j i", i=4, j=PACK),
                 raw[:].rearrange("p j (c i) -> p c j i", i=4),
                 share,
             )
@@ -116,18 +129,18 @@ def tile_moe_res_glu_relu_kernel(tc, xT, xr, w1, w3, w2, gate, offs, out):
             quantize(w_codes[c][:], w_scales[c][:], w_bf[c][:])
 
         def tokens_to_slots(s):
-            cast_rows(x_bf[s], x_raw[s], X_SHARE)
+            cast_rows(x_bf[s][:], x_raw[s], X_SHARE)
             for lo in (HALF, 0):
                 cols = slice(lo, lo + HALF)
                 quantize(x_words[s][:, cols], x_bytes[4 * s : P, cols], x_bf[s][:, lo * PACK : (lo + HALF) * PACK])
             nc.vector.tensor_copy(slot_words[s][:], x_words[s][:].indirect(offsets[:]))
 
-        def first_layer(e, g):
+        def first_layer(e, g, bank_numbers, t_order=range(PACK)):
             banks = []
             for b in range(BLOCKS):
-                bank = psum.tile([P, PACK, BLK], F32, name="bank")
+                bank = bank_tile(bank_numbers[b], [P, PACK, BLK])
                 slots = slice(e * C + b * BLK, e * C + (b + 1) * BLK)
-                for t in range(PACK):
+                for t in t_order:
                     cols = slice(t * P, (t + 1) * P)
                     for s in range(PASSES):
                         nc.tensor.matmul_mx(
@@ -157,8 +170,8 @@ def tile_moe_res_glu_relu_kernel(tc, xT, xr, w1, w3, w2, gate, offs, out):
         def gated(h_bf, bank, relu_values):
             nc.vector.tensor_tensor(in_runs(h_bf), by_slot(bank), relu_values, MULT)
 
-        def second_layer(e, lo, hi):
-            bank = psum.tile([P, hi - lo], F32, name="bank")
+        def second_layer(e, lo, hi, bank_number):
+            bank = bank_tile(bank_number, [P, hi - lo])
             nc.tensor.matmul_mx(
                 out=bank[:],
                 lhsT=w2_codes[e][:].bitcast(FP8X4),
@@ -181,11 +194,11 @@ def tile_moe_res_glu_relu_kernel(tc, xT, xr, w1, w3, w2, gate, offs, out):
         cast_chunk((FIRST, W1, 1), W_SHARE)
         for s in range(PASSES):
             quantize_chunk((FIRST, W1, s))
-        a_first = first_layer(FIRST, W1)
+        a_first = first_layer(FIRST, W1, (0, 1))
         for s in range(PASSES):
             cast_chunk((FIRST, W3, s), W_SHARE)
             quantize_chunk((FIRST, W3, s))
-        b_first = first_layer(FIRST, W3)
+        b_first = first_layer(FIRST, W3, (2, 3))
 
         h_first = sbuf("h_first", [P, C * PACK], BF16)
         relu(cast_part((FIRST, W3, 1)), a_first[0])
@@ -195,50 +208,40 @@ def tile_moe_res_glu_relu_kernel(tc, xT, xr, w1, w3, w2, gate, offs, out):
         relu(cast_part((LAST, W1, 0)), a_first[1])
         cast_rows(w2_bf[FIRST], w2_raw[FIRST], N // 4)
         gated(h_first[:, BLK * PACK :], b_first[1], cast_part((LAST, W1, 0)))
-        cast_chunk((LAST, W1, 1), W_SHARE)
-        quantize(w2_codes[FIRST][:], w2_scales[FIRST][:], w2_bf[FIRST][:])
+        quantize(w2_codes[FIRST][:], w2_scales[FIRST][:], w2_bf[FIRST])
         quantize(h_codes[FIRST][:], h_scales[FIRST][:], h_first[:])
+        y_first = second_layer(FIRST, 0, C, 4)
+        cast_chunk((LAST, W1, 1), W_SHARE)
         quantize_chunk((LAST, W1, 1))
-        y_first = second_layer(FIRST, 0, C)
-        a_last = first_layer(LAST, W1)
+        a_last = first_layer(LAST, W1, (5, 6))
         y_early = sbuf("y_early", [P, BLK], F32)
         nc.scalar.activation(y_early[:], y_first[:, :BLK], COPY)
-        cast_chunk((LAST, W3, 0), W_SHARE)
+        cast_chunk((LAST, W3, 0), W_SHARE_BUSY)
         scatter(FIRST, 0, BLK, y_early[:], gate_sb[FIRST, 0][:])
         quantize_chunk((LAST, W3, 0))
-        warm = psum.tile([P, S], F32, name="bank")
-        for u in range(WARM_UPS):
-            nc.tensor.matmul_mx(
-                out=warm[:],
-                lhsT=w_codes[LAST, W3, 0][:, :P].bitcast(FP8X4),
-                lhsT_scale=w_scales[LAST, W3, 0][:, :P],
-                rhs=slot_words[0][:].bitcast(FP8X4),
-                rhs_scale=slot_bytes[:],
-                start=True,
-                stop=True,
-            )
-        cast_chunk((LAST, W3, 1), W_SHARE_URGENT)
-        quantize_chunk((LAST, W3, 1))
-        b_last = first_layer(LAST, W3)
 
-        late = sbuf("w_raw%d%d%d" % chunks[-1], [P, C + BLOCKS * BLK * PACK], F32)
-        relu_last = [late[:, C + b * BLK * PACK : C + (b + 1) * BLK * PACK] for b in range(BLOCKS)]
-        nc.scalar.activation(late[:, :BLK], y_first[:, BLK:], COPY)
-        scatter(FIRST, BLK, C, late[:, :BLK], gate_sb[FIRST, BLK][:])
-        for b in range(BLOCKS):
-            relu(in_runs(relu_last[b]), a_last[b])
+        end_src = w_raw[end][:].rearrange("p j (m t) -> p m j t", t=PACK)
+        nc.vector.tensor_copy(end_upper.rearrange("p (t m j) -> p m j t", t=2, j=PACK), end_src[:, :, :, 2:])
+        cast(end_lower.rearrange("p (t m j) -> p m j t", t=2, j=PACK), end_src[:, :, :, :2], END_SHARE)
+        quantize(w_codes[end][:, H // 2 :], w_scales[end][:, H // 2 :], end_upper)
+        quantize(w_codes[end][:, : H // 2], w_scales[end][:, : H // 2], end_lower)
+        nc.scalar.activation(y_late, y_first[:, BLK:], COPY)
+        scatter(FIRST, BLK, C, y_late, gate_sb[FIRST, BLK][:])
+        relu(in_runs(relu_last[0]), a_last[0])
         cast_rows(w2_bf[LAST], w2_raw[LAST], N // 4)
+        relu(in_runs(relu_last[1]), a_last[1])
+        b_last = first_layer(LAST, W3, (7, 5), (2, 3, 0, 1))
 
-        h_last = [sbuf("h_last", [P, BLK * PACK], BF16)[:], w2_bf[LAST][:]]
+        h_last = [sbuf("h_last", [P, BLK * PACK], BF16)[:], w2_bf[LAST]]
         y_last = [relu_last[1][:, :BLK], sbuf("y_last", [P, BLK], F32)[:]]
         gated(h_last[0], b_last[0], in_runs(relu_last[0]))
-        quantize(w2_codes[LAST][:], w2_scales[LAST][:], w2_bf[LAST][:])
+        quantize(w2_codes[LAST][:], w2_scales[LAST][:], w2_bf[LAST])
         quantize(h_codes[LAST][:, :BLK], h_scales[LAST][:, :BLK], h_last[0])
-        y_bank = second_layer(LAST, 0, BLK)
+        y_bank = second_layer(LAST, 0, BLK, 0)
         gated(h_last[1], b_last[1], in_runs(relu_last[1]))
         nc.scalar.activation(y_last[0], y_bank[:], COPY)
         quantize(h_codes[LAST][:, BLK:], h_scales[LAST][:, BLK:], h_last[1])
-        y_bank = second_layer(LAST, BLK, C)
+        y_bank = second_layer(LAST, BLK, C, 1)
         scatter(LAST, 0, BLK, y_last[0], gate_sb[LAST, 0][:, :BLK])
         nc.scalar.activation(y_last[1], y_bank[:], COPY)
         scatter(LAST, BLK, C, y_last[1], gate_sb[LAST, 0][:, BLK:])

@@ -19,7 +19,8 @@ FIRST, LAST = 0, 1
 X_SHARE = 112
 W_SHARE = 64
 W_SHARE_URGENT = 40
-W_SHARE_BUSY = 56
+W_SHARE_GATHER = 112
+W_SHARE_LATE = 72
 END_SHARE = 96
 
 END = H * PACK // 2
@@ -66,11 +67,11 @@ def tile_moe_res_glu_relu_kernel(tc, xT, xr, w1, w3, w2, gate, offs, out):
         w_scales = {c: sbuf("w_scales%d%d%d" % c, [P, H], U8) for c in chunks}
         w2_raw = [sbuf(f"w2_raw{e}", [P, PACK, N], F32) for e in range(E)]
         upper = sbuf("upper", [P, 2 * (BLK + BLK * PACK)], BF16)
-        lower = sbuf("lower", [P, N * PACK + 2 * BLK * PACK], BF16)
+        lower = sbuf("lower", [P, N * PACK - LAP + END], BF16)
         end_upper = upper[:, 2 * BLK - LAP : 2 * BLK - LAP + END]
-        end_lower = lower[:, N * PACK - LAP : N * PACK - LAP + END]
+        end_lower = lower[:, N * PACK - LAP :]
         y_late = upper[:, : 2 * BLK].bitcast(F32)
-        relu_last = [upper[:, 2 * BLK :].bitcast(F32), lower[:, N * PACK :].bitcast(F32)]
+        relu_late = upper[:, 2 * BLK :].bitcast(F32)
         w2_bf = [sbuf("w2_bf0", [P, N * PACK], BF16)[:], lower[:, : N * PACK]]
         w2_codes = [sbuf(f"w2_codes{e}", [P, N], U32) for e in range(E)]
         w2_scales = [sbuf(f"w2_scales{e}", [P, N], U8) for e in range(E)]
@@ -128,11 +129,16 @@ def tile_moe_res_glu_relu_kernel(tc, xT, xr, w1, w3, w2, gate, offs, out):
         def quantize_chunk(c):
             quantize(w_codes[c][:], w_scales[c][:], w_bf[c][:])
 
-        def tokens_to_slots(s):
-            cast_rows(x_bf[s][:], x_raw[s], X_SHARE)
+        def quantize_tokens(s):
+            dst = x_bf[s][:].rearrange("p (c i j) -> p c j i", i=4, j=PACK)
+            src = x_raw[s][:].rearrange("p j (c i) -> p c j i", i=4)
+            nc.vector.tensor_copy(dst[:, HALF // 4 :], src[:, HALF // 4 :])
+            cast(dst[:, : HALF // 4], src[:, : HALF // 4], X_SHARE)
             for lo in (HALF, 0):
                 cols = slice(lo, lo + HALF)
                 quantize(x_words[s][:, cols], x_bytes[4 * s : P, cols], x_bf[s][:, lo * PACK : (lo + HALF) * PACK])
+
+        def gather_words(s):
             nc.vector.tensor_copy(slot_words[s][:], x_words[s][:].indirect(offsets[:]))
 
         def first_layer(e, g, bank_numbers, t_order=range(PACK)):
@@ -187,9 +193,11 @@ def tile_moe_res_glu_relu_kernel(tc, xT, xr, w1, w3, w2, gate, offs, out):
             entries = offsets[:, (e * C + lo) // 16 : (e * C + hi) // 16]
             nc.vector.tensor_tensor(window[:].indirect(entries), y, gates, MULT)
 
-        tokens_to_slots(0)
-        tokens_to_slots(1)
-        cast_chunk((FIRST, W1, 0), P)
+        quantize_tokens(0)
+        gather_words(0)
+        quantize_tokens(1)
+        cast_chunk((FIRST, W1, 0), W_SHARE_GATHER)
+        gather_words(1)
         nc.vector.tensor_copy(slot_bytes[:], x_bytes[:].indirect(offsets[:]))
         cast_chunk((FIRST, W1, 1), W_SHARE)
         for s in range(PASSES):
@@ -211,14 +219,15 @@ def tile_moe_res_glu_relu_kernel(tc, xT, xr, w1, w3, w2, gate, offs, out):
         quantize(w2_codes[FIRST][:], w2_scales[FIRST][:], w2_bf[FIRST])
         quantize(h_codes[FIRST][:], h_scales[FIRST][:], h_first[:])
         y_first = second_layer(FIRST, 0, C, 4)
-        cast_chunk((LAST, W1, 1), W_SHARE)
+        cast_chunk((LAST, W1, 1), W_SHARE_LATE)
         quantize_chunk((LAST, W1, 1))
         a_last = first_layer(LAST, W1, (5, 6))
         y_early = sbuf("y_early", [P, BLK], F32)
         nc.scalar.activation(y_early[:], y_first[:, :BLK], COPY)
-        cast_chunk((LAST, W3, 0), W_SHARE_BUSY)
+        cast_chunk((LAST, W3, 0), W_SHARE_LATE)
         scatter(FIRST, 0, BLK, y_early[:], gate_sb[FIRST, 0][:])
         quantize_chunk((LAST, W3, 0))
+        relu(cast_part((LAST, W3, 0)), a_last[0])
 
         end_src = w_raw[end][:].rearrange("p j (m t) -> p m j t", t=PACK)
         nc.vector.tensor_copy(end_upper.rearrange("p (t m j) -> p m j t", t=2, j=PACK), end_src[:, :, :, 2:])
@@ -227,18 +236,17 @@ def tile_moe_res_glu_relu_kernel(tc, xT, xr, w1, w3, w2, gate, offs, out):
         quantize(w_codes[end][:, : H // 2], w_scales[end][:, : H // 2], end_lower)
         nc.scalar.activation(y_late, y_first[:, BLK:], COPY)
         scatter(FIRST, BLK, C, y_late, gate_sb[FIRST, BLK][:])
-        relu(in_runs(relu_last[0]), a_last[0])
+        relu(in_runs(relu_late), a_last[1])
         cast_rows(w2_bf[LAST], w2_raw[LAST], N // 4)
-        relu(in_runs(relu_last[1]), a_last[1])
-        b_last = first_layer(LAST, W3, (7, 5), (2, 3, 0, 1))
+        b_last = first_layer(LAST, W3, (7, 6), (2, 3, 0, 1))
 
         h_last = [sbuf("h_last", [P, BLK * PACK], BF16)[:], w2_bf[LAST]]
-        y_last = [relu_last[1][:, :BLK], sbuf("y_last", [P, BLK], F32)[:]]
-        gated(h_last[0], b_last[0], in_runs(relu_last[0]))
+        y_last = [relu_late[:, :BLK], sbuf("y_last", [P, BLK], F32)[:]]
+        gated(h_last[0], b_last[0], cast_part((LAST, W3, 0)))
         quantize(w2_codes[LAST][:], w2_scales[LAST][:], w2_bf[LAST])
         quantize(h_codes[LAST][:, :BLK], h_scales[LAST][:, :BLK], h_last[0])
         y_bank = second_layer(LAST, 0, BLK, 0)
-        gated(h_last[1], b_last[1], in_runs(relu_last[1]))
+        gated(h_last[1], b_last[1], in_runs(relu_late))
         nc.scalar.activation(y_last[0], y_bank[:], COPY)
         quantize(h_codes[LAST][:, BLK:], h_scales[LAST][:, BLK:], h_last[1])
         y_bank = second_layer(LAST, BLK, C, 1)
@@ -246,8 +254,8 @@ def tile_moe_res_glu_relu_kernel(tc, xT, xr, w1, w3, w2, gate, offs, out):
         nc.scalar.activation(y_last[1], y_bank[:], COPY)
         scatter(LAST, BLK, C, y_last[1], gate_sb[LAST, 0][:, BLK:])
 
-        for lo in (0, HALF):
-            cols = slice(lo, lo + HALF)
-            out_sb = sbuf(f"out{lo}", [P, HALF], F32)
+        for lo in range(0, T, T // 4):
+            cols = slice(lo, lo + T // 4)
+            out_sb = sbuf(f"out{lo}", [P, T // 4], F32)
             nc.vector.tensor_tensor(out_sb[:], window[:, cols], xr_sb[:, cols], ADD)
             nc.sync.dma_start(out[:, cols], out_sb[:])

@@ -17,15 +17,14 @@ W1, W3 = 0, 1
 FIRST, LAST = 0, 1
 
 X_SHARE = 112
-W_SHARE = 64
-W_SHARE_URGENT = 40
+W_SHARE = 88
+W_SHARE_URGENT = 48
 W_SHARE_GATHER = 112
-W_SHARE_LATE = 72
+W_SHARE_LATE = 60
 END_SHARE = 96
 
 END = H * PACK // 2
-LAP = 32
-GATE_PARTS = ((FIRST, 0, BLK), (FIRST, BLK, C), (LAST, 0, C))
+LAP = 16
 
 F32 = mybir.dt.float32
 BF16 = mybir.dt.bfloat16
@@ -61,23 +60,23 @@ def tile_moe_res_glu_relu_kernel(tc, xT, xr, w1, w3, w2, gate, offs, out):
         x_bytes = sbuf("x_bytes", [P, T], U8)
         slot_words = [sbuf(f"slot_words{s}", [P, S], U32) for s in range(PASSES)]
         slot_bytes = sbuf("slot_bytes", [P, S], U8)
-        w_raw = {c: sbuf("w_raw%d%d%d" % c, [P, PACK, H], F32) for c in chunks}
+        w_raw = {c: sbuf("w_raw%d%d%d" % c, [P, PACK, H], F32)[:] for c in chunks if c != (LAST, W1, 0)}
+        h_start = PACK * H - BLK * PACK // 2 - LAP
+        shared = sbuf("shared", [P, h_start + C * PACK // 2], F32)
+        w_raw[LAST, W1, 0] = shared[:, : PACK * H].rearrange("p (j w) -> p j w", j=PACK)
+        h_first = shared[:, h_start:].bitcast(BF16)
         w_bf = {c: sbuf("w_bf%d%d%d" % c, [P, H * PACK], BF16) for c in chunks[:-1]}
         w_codes = {c: sbuf("w_codes%d%d%d" % c, [P, H], U32) for c in chunks}
         w_scales = {c: sbuf("w_scales%d%d%d" % c, [P, H], U8) for c in chunks}
         w2_raw = [sbuf(f"w2_raw{e}", [P, PACK, N], F32) for e in range(E)]
-        upper = sbuf("upper", [P, 2 * (BLK + BLK * PACK)], BF16)
-        lower = sbuf("lower", [P, N * PACK - LAP + END], BF16)
-        end_upper = upper[:, 2 * BLK - LAP : 2 * BLK - LAP + END]
-        end_lower = lower[:, N * PACK - LAP :]
-        y_late = upper[:, : 2 * BLK].bitcast(F32)
-        relu_late = upper[:, 2 * BLK :].bitcast(F32)
-        w2_bf = [sbuf("w2_bf0", [P, N * PACK], BF16)[:], lower[:, : N * PACK]]
+        end_upper = sbuf("end_upper", [P, END], BF16)[:]
+        end_lower = sbuf("end_lower", [P, END], BF16)[:]
+        w2_bf = [sbuf(f"w2_bf{e}", [P, N * PACK], BF16)[:] for e in range(E)]
         w2_codes = [sbuf(f"w2_codes{e}", [P, N], U32) for e in range(E)]
         w2_scales = [sbuf(f"w2_scales{e}", [P, N], U8) for e in range(E)]
         h_codes = [sbuf(f"h_codes{e}", [P, C], U32) for e in range(E)]
         h_scales = [sbuf(f"h_scales{e}", [P, C], U8) for e in range(E)]
-        gate_sb = {(e, lo): sbuf(f"gate{e}_{lo}", [P, hi - lo], F32) for e, lo, hi in GATE_PARTS}
+        gate_sb = [sbuf(f"gate{e}", [P, C], F32) for e in range(E)]
         xr_sb = sbuf("xr", [P, T], F32)
         window = sbuf("window", [P, T], F32)
 
@@ -85,23 +84,21 @@ def tile_moe_res_glu_relu_kernel(tc, xT, xr, w1, w3, w2, gate, offs, out):
         nc.gpsimd.memset(window[:], 0.0)
 
         def load_rows(tile, rows):
-            nc.sync.dma_start(tile[:], rows.rearrange("(p j) w -> p j w", j=PACK))
+            nc.sync.dma_start(tile, rows.rearrange("(p j) w -> p j w", j=PACK))
 
         def load_chunk(e, g, s):
             load_rows(w_raw[e, g, s], (w1, w3)[g][e][s * K_PASS : (s + 1) * K_PASS, :])
 
-        load_rows(x_raw[0], xT[:K_PASS, :])
+        load_rows(x_raw[0][:], xT[:K_PASS, :])
         nc.sync.dma_start(offsets[:], offs)
-        load_rows(x_raw[1], xT[K_PASS:, :])
+        load_rows(x_raw[1][:], xT[K_PASS:, :])
         for c in chunks:
             load_chunk(*c)
             if c == (LAST, W1, 0):
-                load_rows(w2_raw[FIRST], w2[FIRST])
-            if c == (LAST, W3, 0):
-                nc.sync.dma_start(gate_sb[FIRST, 0][:], gate[:, :BLK])
-        nc.sync.dma_start(gate_sb[FIRST, BLK][:], gate[:, BLK:C])
-        load_rows(w2_raw[LAST], w2[LAST])
-        nc.sync.dma_start(gate_sb[LAST, 0][:], gate[:, C:])
+                load_rows(w2_raw[FIRST][:], w2[FIRST])
+        load_rows(w2_raw[LAST][:], w2[LAST])
+        for e in range(E):
+            nc.sync.dma_start(gate_sb[e][:], gate[:, e * C : (e + 1) * C])
         nc.sync.dma_start(xr_sb[:], xr)
 
         def cast(dst, src, share):
@@ -119,7 +116,7 @@ def tile_moe_res_glu_relu_kernel(tc, xT, xr, w1, w3, w2, gate, offs, out):
         def cast_chunk(c, share):
             cast(
                 w_bf[c][:].rearrange("p (t m j) -> p m j t", t=PACK, j=PACK),
-                w_raw[c][:].rearrange("p j (m t) -> p m j t", t=PACK),
+                w_raw[c].rearrange("p j (m t) -> p m j t", t=PACK),
                 share,
             )
 
@@ -142,23 +139,21 @@ def tile_moe_res_glu_relu_kernel(tc, xT, xr, w1, w3, w2, gate, offs, out):
             nc.vector.tensor_copy(slot_words[s][:], x_words[s][:].indirect(offsets[:]))
 
         def first_layer(e, g, bank_numbers, t_order=range(PACK)):
-            banks = []
-            for b in range(BLOCKS):
-                bank = bank_tile(bank_numbers[b], [P, PACK, BLK])
-                slots = slice(e * C + b * BLK, e * C + (b + 1) * BLK)
-                for t in t_order:
-                    cols = slice(t * P, (t + 1) * P)
-                    for s in range(PASSES):
+            banks = [bank_tile(number, [P, PACK, BLK]) for number in bank_numbers]
+            for s in range(PASSES):
+                for b in range(BLOCKS):
+                    slots = slice(e * C + b * BLK, e * C + (b + 1) * BLK)
+                    for place, t in enumerate(t_order):
+                        cols = slice(t * P, (t + 1) * P)
                         nc.tensor.matmul_mx(
-                            out=bank[:, t, :],
+                            out=banks[b][:, t, :],
                             lhsT=w_codes[e, g, s][:, cols].bitcast(FP8X4),
                             lhsT_scale=w_scales[e, g, s][:, cols],
                             rhs=slot_words[s][:, slots].bitcast(FP8X4),
                             rhs_scale=slot_bytes[4 * s : P, slots],
-                            start=(s == 0),
-                            stop=(s == PASSES - 1),
+                            start=(s == 0 and place == 0),
+                            stop=(s == PASSES - 1 and place == PACK - 1),
                         )
-                banks.append(bank)
             return banks
 
         def by_slot(bank):
@@ -167,8 +162,8 @@ def tile_moe_res_glu_relu_kernel(tc, xT, xr, w1, w3, w2, gate, offs, out):
         def in_runs(flat):
             return flat.rearrange("p (r n t) -> p r n t", r=4, t=PACK)
 
-        def cast_part(c):
-            return w_raw[c][:, :, :BLK].rearrange("p r (n t) -> p r n t", t=PACK)
+        def cast_part(c, lo=0):
+            return w_raw[c][:, :, lo : lo + BLK].rearrange("p r (n t) -> p r n t", t=PACK)
 
         def relu(dst, bank):
             nc.scalar.activation(dst, by_slot(bank), RELU)
@@ -203,56 +198,59 @@ def tile_moe_res_glu_relu_kernel(tc, xT, xr, w1, w3, w2, gate, offs, out):
         for s in range(PASSES):
             quantize_chunk((FIRST, W1, s))
         a_first = first_layer(FIRST, W1, (0, 1))
-        for s in range(PASSES):
-            cast_chunk((FIRST, W3, s), W_SHARE)
-            quantize_chunk((FIRST, W3, s))
+        cast_chunk((FIRST, W3, 0), W_SHARE)
+        quantize_chunk((FIRST, W3, 0))
+        cast_chunk((FIRST, W3, 1), W_SHARE_URGENT)
+        quantize_chunk((FIRST, W3, 1))
+        relu_first = [cast_part((FIRST, W3, 1), lo) for lo in (0, H - BLK)]
+        for b in range(BLOCKS):
+            relu(relu_first[b], a_first[b])
         b_first = first_layer(FIRST, W3, (2, 3))
 
-        h_first = sbuf("h_first", [P, C * PACK], BF16)
-        relu(cast_part((FIRST, W3, 1)), a_first[0])
-        cast_chunk((LAST, W1, 0), W_SHARE_URGENT)
+        cast_chunk((LAST, W1, 0), W_SHARE_LATE)
+        gated(h_first[:, : BLK * PACK], b_first[0], relu_first[0])
+        gated(h_first[:, BLK * PACK :], b_first[1], relu_first[1])
         quantize_chunk((LAST, W1, 0))
-        gated(h_first[:, : BLK * PACK], b_first[0], cast_part((FIRST, W3, 1)))
-        relu(cast_part((LAST, W1, 0)), a_first[1])
         cast_rows(w2_bf[FIRST], w2_raw[FIRST], N // 4)
-        gated(h_first[:, BLK * PACK :], b_first[1], cast_part((LAST, W1, 0)))
+        quantize(h_codes[FIRST][:], h_scales[FIRST][:], h_first)
         quantize(w2_codes[FIRST][:], w2_scales[FIRST][:], w2_bf[FIRST])
-        quantize(h_codes[FIRST][:], h_scales[FIRST][:], h_first[:])
         y_first = second_layer(FIRST, 0, C, 4)
-        cast_chunk((LAST, W1, 1), W_SHARE_LATE)
+        cast_chunk((LAST, W1, 1), W_SHARE_URGENT)
         quantize_chunk((LAST, W1, 1))
         a_last = first_layer(LAST, W1, (5, 6))
         y_early = sbuf("y_early", [P, BLK], F32)
         nc.scalar.activation(y_early[:], y_first[:, :BLK], COPY)
-        cast_chunk((LAST, W3, 0), W_SHARE_LATE)
-        scatter(FIRST, 0, BLK, y_early[:], gate_sb[FIRST, 0][:])
+        cast_chunk((LAST, W3, 0), W_SHARE_URGENT)
         quantize_chunk((LAST, W3, 0))
-        relu(cast_part((LAST, W3, 0)), a_last[0])
+        relu_last = [cast_part((LAST, W3, 0), lo) for lo in (0, H - BLK)]
+        for b in range(BLOCKS):
+            relu(relu_last[b], a_last[b])
 
-        end_src = w_raw[end][:].rearrange("p j (m t) -> p m j t", t=PACK)
+        end_src = w_raw[end].rearrange("p j (m t) -> p m j t", t=PACK)
         nc.vector.tensor_copy(end_upper.rearrange("p (t m j) -> p m j t", t=2, j=PACK), end_src[:, :, :, 2:])
         cast(end_lower.rearrange("p (t m j) -> p m j t", t=2, j=PACK), end_src[:, :, :, :2], END_SHARE)
         quantize(w_codes[end][:, H // 2 :], w_scales[end][:, H // 2 :], end_upper)
         quantize(w_codes[end][:, : H // 2], w_scales[end][:, : H // 2], end_lower)
-        nc.scalar.activation(y_late, y_first[:, BLK:], COPY)
-        scatter(FIRST, BLK, C, y_late, gate_sb[FIRST, BLK][:])
-        relu(in_runs(relu_late), a_last[1])
+        b_last = first_layer(LAST, W3, (7, 0), (2, 3, 0, 1))
+        scatter(FIRST, 0, BLK, y_early[:], gate_sb[FIRST][:, :BLK])
         cast_rows(w2_bf[LAST], w2_raw[LAST], N // 4)
-        b_last = first_layer(LAST, W3, (7, 6), (2, 3, 0, 1))
 
-        h_last = [sbuf("h_last", [P, BLK * PACK], BF16)[:], w2_bf[LAST]]
-        y_last = [relu_late[:, :BLK], sbuf("y_last", [P, BLK], F32)[:]]
-        gated(h_last[0], b_last[0], cast_part((LAST, W3, 0)))
+        h_last = sbuf("h_last", [P, C * PACK], BF16)
+        gated(h_last[:, : BLK * PACK], b_last[0], relu_last[0])
+        gated(h_last[:, BLK * PACK :], b_last[1], relu_last[1])
         quantize(w2_codes[LAST][:], w2_scales[LAST][:], w2_bf[LAST])
-        quantize(h_codes[LAST][:, :BLK], h_scales[LAST][:, :BLK], h_last[0])
-        y_bank = second_layer(LAST, 0, BLK, 0)
-        gated(h_last[1], b_last[1], in_runs(relu_late))
-        nc.scalar.activation(y_last[0], y_bank[:], COPY)
-        quantize(h_codes[LAST][:, BLK:], h_scales[LAST][:, BLK:], h_last[1])
-        y_bank = second_layer(LAST, BLK, C, 1)
-        scatter(LAST, 0, BLK, y_last[0], gate_sb[LAST, 0][:, :BLK])
-        nc.scalar.activation(y_last[1], y_bank[:], COPY)
-        scatter(LAST, BLK, C, y_last[1], gate_sb[LAST, 0][:, BLK:])
+        y_banks = []
+        for b in range(BLOCKS):
+            slots = slice(b * BLK, (b + 1) * BLK)
+            quantize(h_codes[LAST][:, slots], h_scales[LAST][:, slots], h_last[:, b * BLK * PACK : (b + 1) * BLK * PACK])
+            y_banks.append(second_layer(LAST, b * BLK, (b + 1) * BLK, 1 + b))
+        y_late = w_raw[LAST, W3, 0][:, 0, H - BLK :]
+        nc.scalar.activation(y_late, y_first[:, BLK:], COPY)
+        scatter(FIRST, BLK, C, y_late, gate_sb[FIRST][:, BLK:])
+        y_last = sbuf("y_last", [P, C], F32)
+        for b in range(BLOCKS):
+            nc.scalar.activation(y_last[:, b * BLK : (b + 1) * BLK], y_banks[b][:], COPY)
+        scatter(LAST, 0, C, y_last[:], gate_sb[LAST][:])
 
         for lo in range(0, T, T // 4):
             cols = slice(lo, lo + T // 4)

@@ -16,12 +16,12 @@ HALF = T // 2
 W1, W3 = 0, 1
 FIRST, LAST = 0, 1
 
-X_SHARE = 112
-W_SHARE = 88
+X_SHARE = 104
+W_SHARE = 80
 W_SHARE_URGENT = 48
-W_SHARE_GATHER = 112
-W_SHARE_LATE = 60
-END_SHARE = 96
+W_SHARE_GATHER = 104
+W_SHARE_LATE = 70
+END_SHARE = 80
 
 END = H * PACK // 2
 LAP = 16
@@ -94,9 +94,8 @@ def tile_moe_res_glu_relu_kernel(tc, xT, xr, w1, w3, w2, gate, offs, out):
         load_rows(x_raw[1][:], xT[K_PASS:, :])
         for c in chunks:
             load_chunk(*c)
-            if c == (LAST, W1, 0):
-                load_rows(w2_raw[FIRST][:], w2[FIRST])
-        load_rows(w2_raw[LAST][:], w2[LAST])
+        for e in range(E):
+            load_rows(w2_raw[e][:], w2[e])
         for e in range(E):
             nc.sync.dma_start(gate_sb[e][:], gate[:, e * C : (e + 1) * C])
         nc.sync.dma_start(xr_sb[:], xr)
@@ -211,15 +210,10 @@ def tile_moe_res_glu_relu_kernel(tc, xT, xr, w1, w3, w2, gate, offs, out):
         gated(h_first[:, : BLK * PACK], b_first[0], relu_first[0])
         gated(h_first[:, BLK * PACK :], b_first[1], relu_first[1])
         quantize_chunk((LAST, W1, 0))
-        cast_rows(w2_bf[FIRST], w2_raw[FIRST], N // 4)
+        cast_chunk((LAST, W1, 1), W_SHARE_LATE)
         quantize(h_codes[FIRST][:], h_scales[FIRST][:], h_first)
-        quantize(w2_codes[FIRST][:], w2_scales[FIRST][:], w2_bf[FIRST])
-        y_first = second_layer(FIRST, 0, C, 4)
-        cast_chunk((LAST, W1, 1), W_SHARE_URGENT)
         quantize_chunk((LAST, W1, 1))
         a_last = first_layer(LAST, W1, (5, 6))
-        y_early = sbuf("y_early", [P, BLK], F32)
-        nc.scalar.activation(y_early[:], y_first[:, :BLK], COPY)
         cast_chunk((LAST, W3, 0), W_SHARE_URGENT)
         quantize_chunk((LAST, W3, 0))
         relu_last = [cast_part((LAST, W3, 0), lo) for lo in (0, H - BLK)]
@@ -232,8 +226,12 @@ def tile_moe_res_glu_relu_kernel(tc, xT, xr, w1, w3, w2, gate, offs, out):
         quantize(w_codes[end][:, H // 2 :], w_scales[end][:, H // 2 :], end_upper)
         quantize(w_codes[end][:, : H // 2], w_scales[end][:, : H // 2], end_lower)
         b_last = first_layer(LAST, W3, (7, 0), (2, 3, 0, 1))
-        scatter(FIRST, 0, BLK, y_early[:], gate_sb[FIRST][:, :BLK])
-        cast_rows(w2_bf[LAST], w2_raw[LAST], N // 4)
+        for e in range(E):
+            cast_rows(w2_bf[e], w2_raw[e], N // 4)
+        quantize(w2_codes[FIRST][:], w2_scales[FIRST][:], w2_bf[FIRST])
+        y_first = second_layer(FIRST, 0, C, 4)
+        y_late = sbuf("y_first", [P, C], F32)
+        nc.scalar.activation(y_late[:], y_first[:], COPY)
 
         h_last = sbuf("h_last", [P, C * PACK], BF16)
         gated(h_last[:, : BLK * PACK], b_last[0], relu_last[0])
@@ -244,9 +242,7 @@ def tile_moe_res_glu_relu_kernel(tc, xT, xr, w1, w3, w2, gate, offs, out):
             slots = slice(b * BLK, (b + 1) * BLK)
             quantize(h_codes[LAST][:, slots], h_scales[LAST][:, slots], h_last[:, b * BLK * PACK : (b + 1) * BLK * PACK])
             y_banks.append(second_layer(LAST, b * BLK, (b + 1) * BLK, 1 + b))
-        y_late = w_raw[LAST, W3, 0][:, 0, H - BLK :]
-        nc.scalar.activation(y_late, y_first[:, BLK:], COPY)
-        scatter(FIRST, BLK, C, y_late, gate_sb[FIRST][:, BLK:])
+        scatter(FIRST, 0, C, y_late[:], gate_sb[FIRST][:])
         y_last = sbuf("y_last", [P, C], F32)
         for b in range(BLOCKS):
             nc.scalar.activation(y_last[:, b * BLK : (b + 1) * BLK], y_banks[b][:], COPY)

@@ -45,7 +45,7 @@ def tile_moe_res_glu_relu_kernel(tc, xT, xr, w1, w3, w2, gate, offs, out):
         psum = ctx.enter_context(tc.psum_pool(name="psum", bufs=1))
 
         def sbuf(name, shape, dtype):
-            return keep.tile(shape, dtype, name=name, tag=name, align_bytes=64)
+            return keep.tile(shape, dtype, name=name, tag=name, align_bytes=256)
 
         def bank_tile(number, shape):
             return psum.tile(shape, F32, name=f"bank{number}", tag=f"bank{number}")
@@ -89,8 +89,8 @@ def tile_moe_res_glu_relu_kernel(tc, xT, xr, w1, w3, w2, gate, offs, out):
         def load_chunk(e, g, s):
             load_rows(w_raw[e, g, s], (w1, w3)[g][e][s * K_PASS : (s + 1) * K_PASS, :])
 
-        load_rows(x_raw[0][:], xT[:K_PASS, :])
         nc.sync.dma_start(offsets[:], offs)
+        load_rows(x_raw[0][:], xT[:K_PASS, :])
         load_rows(x_raw[1][:], xT[K_PASS:, :])
         for c in chunks:
             load_chunk(*c)

@@ -21,7 +21,7 @@ W_SHARE = 80
 W_SHARE_URGENT = 48
 W_SHARE_GATHER = 104
 W_SHARE_LATE = 70
-END_SHARE = 80
+END_SHARE = 88
 
 END = H * PACK // 2
 LAP = 16
@@ -224,8 +224,10 @@ def tile_moe_res_glu_relu_kernel(tc, xT, xr, w1, w3, w2, gate, offs, out):
         nc.vector.tensor_copy(end_upper.rearrange("p (t m j) -> p m j t", t=2, j=PACK), end_src[:, :, :, 2:])
         cast(end_lower.rearrange("p (t m j) -> p m j t", t=2, j=PACK), end_src[:, :, :, :2], END_SHARE)
         quantize(w_codes[end][:, H // 2 :], w_scales[end][:, H // 2 :], end_upper)
-        quantize(w_codes[end][:, : H // 2], w_scales[end][:, : H // 2], end_lower)
-        b_last = first_layer(LAST, W3, (7, 0), (2, 3, 0, 1))
+        for t in (1, 0):
+            cols = slice(t * P, (t + 1) * P)
+            quantize(w_codes[end][:, cols], w_scales[end][:, cols], end_lower[:, t * P * PACK : (t + 1) * P * PACK])
+        b_last = first_layer(LAST, W3, (7, 0), (2, 3, 1, 0))
         for e in range(E):
             cast_rows(w2_bf[e], w2_raw[e], N // 4)
         quantize(w2_codes[FIRST][:], w2_scales[FIRST][:], w2_bf[FIRST])

@@ -19,6 +19,7 @@ FIRST, LAST = 0, 1
 X_SHARE = 104
 W_SHARE = 80
 W_SHARE_URGENT = 48
+W_SHARE_RELUS = 32
 W_SHARE_GATHER = 104
 W_SHARE_LATE = 70
 END_SHARE = 88
@@ -214,7 +215,7 @@ def tile_moe_res_glu_relu_kernel(tc, xT, xr, w1, w3, w2, gate, offs, out):
         quantize(h_codes[FIRST][:], h_scales[FIRST][:], h_first)
         quantize_chunk((LAST, W1, 1))
         a_last = first_layer(LAST, W1, (5, 6))
-        cast_chunk((LAST, W3, 0), W_SHARE_URGENT)
+        cast_chunk((LAST, W3, 0), W_SHARE_RELUS)
         quantize_chunk((LAST, W3, 0))
         relu_last = [cast_part((LAST, W3, 0), lo) for lo in (0, H - BLK)]
         for b in range(BLOCKS):

@@ -22,7 +22,7 @@ W_SHARE_URGENT = 48
 W_SHARE_RELUS = 32
 W_SHARE_GATHER = 104
 W_SHARE_LATE = 70
-END_SHARE = 88
+END_SHARE = 8
 
 END = H * PACK // 2
 LAP = 16
@@ -72,9 +72,10 @@ def tile_moe_res_glu_relu_kernel(tc, xT, xr, w1, w3, w2, gate, offs, out):
         w2_raw = [sbuf(f"w2_raw{e}", [P, PACK, N], F32) for e in range(E)]
         end_upper = sbuf("end_upper", [P, END], BF16)[:]
         end_lower = sbuf("end_lower", [P, END], BF16)[:]
-        w2_bf = [sbuf(f"w2_bf{e}", [P, N * PACK], BF16)[:] for e in range(E)]
+        h_last = sbuf("h_last", [P, C * PACK], BF16)
+        w2_bf = [sbuf("w2_bf0", [P, N * PACK], BF16)[:], h_last[:, BLK * PACK :]]
         w2_codes = [sbuf(f"w2_codes{e}", [P, N], U32) for e in range(E)]
-        w2_scales = [sbuf(f"w2_scales{e}", [P, N], U8) for e in range(E)]
+        w2_scales = [sbuf("w2_scales0", [P, N], U8)[:], w_scales[end][4:P, :N]]
         h_codes = [sbuf(f"h_codes{e}", [P, C], U32) for e in range(E)]
         h_scales = [sbuf(f"h_scales{e}", [P, C], U8) for e in range(E)]
         gate_sb = [sbuf(f"gate{e}", [P, C], F32) for e in range(E)]
@@ -97,12 +98,12 @@ def tile_moe_res_glu_relu_kernel(tc, xT, xr, w1, w3, w2, gate, offs, out):
             load_chunk(*c)
         for e in range(E):
             load_rows(w2_raw[e][:], w2[e])
-        for e in range(E):
             nc.sync.dma_start(gate_sb[e][:], gate[:, e * C : (e + 1) * C])
         nc.sync.dma_start(xr_sb[:], xr)
 
         def cast(dst, src, share):
-            nc.scalar.activation(dst[:, :share], src[:, :share], COPY)
+            if share > 0:
+                nc.scalar.activation(dst[:, :share], src[:, :share], COPY)
             if share < dst.shape[1]:
                 nc.vector.tensor_copy(dst[:, share:], src[:, share:])
 
@@ -138,22 +139,25 @@ def tile_moe_res_glu_relu_kernel(tc, xT, xr, w1, w3, w2, gate, offs, out):
         def gather_words(s):
             nc.vector.tensor_copy(slot_words[s][:], x_words[s][:].indirect(offsets[:]))
 
-        def first_layer(e, g, bank_numbers, t_order=range(PACK)):
+        def products(e, g, s, b, bank, t_order):
+            slots = slice(e * C + b * BLK, e * C + (b + 1) * BLK)
+            for t in t_order:
+                cols = slice(t * P, (t + 1) * P)
+                nc.tensor.matmul_mx(
+                    out=bank[:, t, :],
+                    lhsT=w_codes[e, g, s][:, cols].bitcast(FP8X4),
+                    lhsT_scale=w_scales[e, g, s][:, cols],
+                    rhs=slot_words[s][:, slots].bitcast(FP8X4),
+                    rhs_scale=slot_bytes[4 * s : P, slots],
+                    start=(s == 0 and t == PACK - 1),
+                    stop=(s == PASSES - 1 and t == 0),
+                )
+
+        def first_layer(e, g, bank_numbers, passes=PASSES):
             banks = [bank_tile(number, [P, PACK, BLK]) for number in bank_numbers]
-            for s in range(PASSES):
+            for s in range(passes):
                 for b in range(BLOCKS):
-                    slots = slice(e * C + b * BLK, e * C + (b + 1) * BLK)
-                    for place, t in enumerate(t_order):
-                        cols = slice(t * P, (t + 1) * P)
-                        nc.tensor.matmul_mx(
-                            out=banks[b][:, t, :],
-                            lhsT=w_codes[e, g, s][:, cols].bitcast(FP8X4),
-                            lhsT_scale=w_scales[e, g, s][:, cols],
-                            rhs=slot_words[s][:, slots].bitcast(FP8X4),
-                            rhs_scale=slot_bytes[4 * s : P, slots],
-                            start=(s == 0 and place == 0),
-                            stop=(s == PASSES - 1 and place == PACK - 1),
-                        )
+                    products(e, g, s, b, banks[b], (3, 2, 1, 0))
             return banks
 
         def by_slot(bank):
@@ -176,7 +180,7 @@ def tile_moe_res_glu_relu_kernel(tc, xT, xr, w1, w3, w2, gate, offs, out):
             nc.tensor.matmul_mx(
                 out=bank[:],
                 lhsT=w2_codes[e][:].bitcast(FP8X4),
-                lhsT_scale=w2_scales[e][:],
+                lhsT_scale=w2_scales[e],
                 rhs=h_codes[e][:, lo:hi].bitcast(FP8X4),
                 rhs_scale=h_scales[e][:, lo:hi],
                 start=True,
@@ -184,9 +188,8 @@ def tile_moe_res_glu_relu_kernel(tc, xT, xr, w1, w3, w2, gate, offs, out):
             )
             return bank
 
-        def scatter(e, lo, hi, y, gates):
-            entries = offsets[:, (e * C + lo) // 16 : (e * C + hi) // 16]
-            nc.vector.tensor_tensor(window[:].indirect(entries), y, gates, MULT)
+        def scattered(e, lo, hi):
+            return window[:].indirect(offsets[:, (e * C + lo) // 16 : (e * C + hi) // 16])
 
         quantize_tokens(0)
         gather_words(0)
@@ -221,35 +224,36 @@ def tile_moe_res_glu_relu_kernel(tc, xT, xr, w1, w3, w2, gate, offs, out):
         for b in range(BLOCKS):
             relu(relu_last[b], a_last[b])
 
+        b_last = first_layer(LAST, W3, (7, 0), 1)
         end_src = w_raw[end].rearrange("p j (m t) -> p m j t", t=PACK)
-        nc.vector.tensor_copy(end_upper.rearrange("p (t m j) -> p m j t", t=2, j=PACK), end_src[:, :, :, 2:])
-        cast(end_lower.rearrange("p (t m j) -> p m j t", t=2, j=PACK), end_src[:, :, :, :2], END_SHARE)
+        cast(end_upper.rearrange("p (t m j) -> p m j t", t=2, j=PACK), end_src[:, :, :, 2:], END_SHARE)
+        cast(end_lower.rearrange("p (t m j) -> p m j t", t=2, j=PACK), end_src[:, :, :, :2], P)
+        cast_rows(w2_bf[FIRST], w2_raw[FIRST], 0)
         quantize(w_codes[end][:, H // 2 :], w_scales[end][:, H // 2 :], end_upper)
+        quantize(w2_codes[FIRST][:], w2_scales[FIRST], w2_bf[FIRST])
         for t in (1, 0):
             cols = slice(t * P, (t + 1) * P)
             quantize(w_codes[end][:, cols], w_scales[end][:, cols], end_lower[:, t * P * PACK : (t + 1) * P * PACK])
-        b_last = first_layer(LAST, W3, (7, 0), (2, 3, 1, 0))
-        for e in range(E):
-            cast_rows(w2_bf[e], w2_raw[e], N // 4)
-        quantize(w2_codes[FIRST][:], w2_scales[FIRST][:], w2_bf[FIRST])
-        y_first = second_layer(FIRST, 0, C, 4)
-        y_late = sbuf("y_first", [P, C], F32)
-        nc.scalar.activation(y_late[:], y_first[:], COPY)
-
-        h_last = sbuf("h_last", [P, C * PACK], BF16)
+        products(LAST, W3, 1, 0, b_last[0], (3, 2))
+        y_bank = second_layer(FIRST, 0, C, 4)
+        products(LAST, W3, 1, 0, b_last[0], (1, 0))
+        products(LAST, W3, 1, 1, b_last[1], (3, 2, 1, 0))
+        cast_rows(w2_bf[LAST], w2_raw[LAST], N // 4)
+        y_first = sbuf("y_first", [P, C], F32)
+        y_last = [sbuf(f"y_last{b}", [P, BLK], F32) for b in range(BLOCKS)]
+        nc.vector.tensor_tensor(y_first[:], y_bank[:], gate_sb[FIRST][:], MULT)
+        nc.scalar.activation(scattered(FIRST, 0, C), y_first[:], COPY)
         gated(h_last[:, : BLK * PACK], b_last[0], relu_last[0])
+        quantize(w2_codes[LAST][:], w2_scales[LAST], w2_bf[LAST])
+        quantize(h_codes[LAST][:, :BLK], h_scales[LAST][:, :BLK], h_last[:, : BLK * PACK])
+        y_bank = second_layer(LAST, 0, BLK, 1)
         gated(h_last[:, BLK * PACK :], b_last[1], relu_last[1])
-        quantize(w2_codes[LAST][:], w2_scales[LAST][:], w2_bf[LAST])
-        y_banks = []
-        for b in range(BLOCKS):
-            slots = slice(b * BLK, (b + 1) * BLK)
-            quantize(h_codes[LAST][:, slots], h_scales[LAST][:, slots], h_last[:, b * BLK * PACK : (b + 1) * BLK * PACK])
-            y_banks.append(second_layer(LAST, b * BLK, (b + 1) * BLK, 1 + b))
-        scatter(FIRST, 0, C, y_late[:], gate_sb[FIRST][:])
-        y_last = sbuf("y_last", [P, C], F32)
-        for b in range(BLOCKS):
-            nc.scalar.activation(y_last[:, b * BLK : (b + 1) * BLK], y_banks[b][:], COPY)
-        scatter(LAST, 0, C, y_last[:], gate_sb[LAST][:])
+        nc.vector.tensor_tensor(y_last[0][:], y_bank[:], gate_sb[LAST][:, :BLK], MULT)
+        quantize(h_codes[LAST][:, BLK:], h_scales[LAST][:, BLK:], h_last[:, BLK * PACK :])
+        y_bank = second_layer(LAST, BLK, C, 2)
+        nc.vector.tensor_copy(scattered(LAST, 0, BLK), y_last[0][:])
+        nc.scalar.activation(y_last[1][:], y_bank[:], COPY)
+        nc.vector.tensor_tensor(scattered(LAST, BLK, C), y_last[1][:], gate_sb[LAST][:, BLK:], MULT)
 
         for lo in range(0, T, T // 4):
             cols = slice(lo, lo + T // 4)

@@ -19,13 +19,14 @@ FIRST, LAST = 0, 1
 X_SHARE = 104
 W_SHARE = 80
 W_SHARE_URGENT = 48
-W_SHARE_RELUS = 32
+W_SHARE_RELUS = 56
 W_SHARE_GATHER = 104
 W_SHARE_LATE = 70
+W_SHARE_SIXTH = 60
 END_SHARE = 8
 
 END = H * PACK // 2
-LAP = 16
+LAP = 64
 
 F32 = mybir.dt.float32
 BF16 = mybir.dt.bfloat16
@@ -61,11 +62,13 @@ def tile_moe_res_glu_relu_kernel(tc, xT, xr, w1, w3, w2, gate, offs, out):
         x_bytes = sbuf("x_bytes", [P, T], U8)
         slot_words = [sbuf(f"slot_words{s}", [P, S], U32) for s in range(PASSES)]
         slot_bytes = sbuf("slot_bytes", [P, S], U8)
-        w_raw = {c: sbuf("w_raw%d%d%d" % c, [P, PACK, H], F32)[:] for c in chunks if c != (LAST, W1, 0)}
-        h_start = PACK * H - BLK * PACK // 2 - LAP
-        shared = sbuf("shared", [P, h_start + C * PACK // 2], F32)
+        w_raw = {c: sbuf("w_raw%d%d%d" % c, [P, PACK, H], F32)[:] for c in chunks if c[:2] != (LAST, W1)}
+        h_start = PACK * H - LAP
+        h_stop = h_start + C * PACK // 2
+        shared = sbuf("shared", [P, h_stop - LAP + PACK * H], F32)
         w_raw[LAST, W1, 0] = shared[:, : PACK * H].rearrange("p (j w) -> p j w", j=PACK)
-        h_first = shared[:, h_start:].bitcast(BF16)
+        w_raw[LAST, W1, 1] = shared[:, h_stop - LAP :].rearrange("p (j w) -> p j w", j=PACK)
+        h_first = shared[:, h_start:h_stop].bitcast(BF16)
         w_bf = {c: sbuf("w_bf%d%d%d" % c, [P, H * PACK], BF16) for c in chunks[:-1]}
         w_codes = {c: sbuf("w_codes%d%d%d" % c, [P, H], U32) for c in chunks}
         w_scales = {c: sbuf("w_scales%d%d%d" % c, [P, H], U8) for c in chunks}
@@ -212,23 +215,26 @@ def tile_moe_res_glu_relu_kernel(tc, xT, xr, w1, w3, w2, gate, offs, out):
 
         cast_chunk((LAST, W1, 0), W_SHARE_LATE)
         gated(h_first[:, : BLK * PACK], b_first[0], relu_first[0])
-        gated(h_first[:, BLK * PACK :], b_first[1], relu_first[1])
         quantize_chunk((LAST, W1, 0))
-        cast_chunk((LAST, W1, 1), W_SHARE_LATE)
-        quantize(h_codes[FIRST][:], h_scales[FIRST][:], h_first)
+        dst = w_bf[LAST, W1, 1][:].rearrange("p (t m j) -> p m j t", t=PACK, j=PACK)
+        src = w_raw[LAST, W1, 1].rearrange("p j (m t) -> p m j t", t=PACK)
+        nc.vector.tensor_copy(dst[:, : P - W_SHARE_SIXTH], src[:, : P - W_SHARE_SIXTH])
+        nc.scalar.activation(dst[:, P - W_SHARE_SIXTH :], src[:, P - W_SHARE_SIXTH :], COPY)
+        gated(h_first[:, BLK * PACK :], b_first[1], relu_first[1])
         quantize_chunk((LAST, W1, 1))
+        quantize(h_codes[FIRST][:], h_scales[FIRST][:], h_first)
         a_last = first_layer(LAST, W1, (5, 6))
         cast_chunk((LAST, W3, 0), W_SHARE_RELUS)
         quantize_chunk((LAST, W3, 0))
-        relu_last = [cast_part((LAST, W3, 0), lo) for lo in (0, H - BLK)]
-        for b in range(BLOCKS):
-            relu(relu_last[b], a_last[b])
+        relu_last = [cast_part((LAST, W3, 0)), w2_raw[FIRST][:].rearrange("p r (n t) -> p r n t", t=PACK)]
+        relu(relu_last[0], a_last[0])
 
         b_last = first_layer(LAST, W3, (7, 0), 1)
         end_src = w_raw[end].rearrange("p j (m t) -> p m j t", t=PACK)
         cast(end_upper.rearrange("p (t m j) -> p m j t", t=2, j=PACK), end_src[:, :, :, 2:], END_SHARE)
         cast(end_lower.rearrange("p (t m j) -> p m j t", t=2, j=PACK), end_src[:, :, :, :2], P)
         cast_rows(w2_bf[FIRST], w2_raw[FIRST], 0)
+        relu(relu_last[1], a_last[1])
         quantize(w_codes[end][:, H // 2 :], w_scales[end][:, H // 2 :], end_upper)
         quantize(w2_codes[FIRST][:], w2_scales[FIRST], w2_bf[FIRST])
         for t in (1, 0):
@@ -259,4 +265,4 @@ def tile_moe_res_glu_relu_kernel(tc, xT, xr, w1, w3, w2, gate, offs, out):
             cols = slice(lo, lo + T // 4)
             out_sb = sbuf(f"out{lo}", [P, T // 4], F32)
             nc.vector.tensor_tensor(out_sb[:], window[:, cols], xr_sb[:, cols], ADD)
-            nc.sync.dma_start(out[:, cols], out_sb[:])
+            (nc.sync, nc.scalar)[lo // (T // 4) % 2].dma_start(out[:, cols], out_sb[:])

@@ -23,10 +23,11 @@ W_SHARE_RELUS = 56
 W_SHARE_GATHER = 104
 W_SHARE_LATE = 70
 W_SHARE_SIXTH = 60
-END_SHARE = 8
 
 END = H * PACK // 2
 LAP = 64
+
+CUTS = (0, 128, 320, 640, T)
 
 F32 = mybir.dt.float32
 BF16 = mybir.dt.bfloat16
@@ -231,7 +232,7 @@ def tile_moe_res_glu_relu_kernel(tc, xT, xr, w1, w3, w2, gate, offs, out):
 
         b_last = first_layer(LAST, W3, (7, 0), 1)
         end_src = w_raw[end].rearrange("p j (m t) -> p m j t", t=PACK)
-        cast(end_upper.rearrange("p (t m j) -> p m j t", t=2, j=PACK), end_src[:, :, :, 2:], END_SHARE)
+        cast(end_upper.rearrange("p (t m j) -> p m j t", t=2, j=PACK), end_src[:, :, :, 2:], 0)
         cast(end_lower.rearrange("p (t m j) -> p m j t", t=2, j=PACK), end_src[:, :, :, :2], P)
         cast_rows(w2_bf[FIRST], w2_raw[FIRST], 0)
         relu(relu_last[1], a_last[1])
@@ -257,12 +258,11 @@ def tile_moe_res_glu_relu_kernel(tc, xT, xr, w1, w3, w2, gate, offs, out):
         nc.vector.tensor_tensor(y_last[0][:], y_bank[:], gate_sb[LAST][:, :BLK], MULT)
         quantize(h_codes[LAST][:, BLK:], h_scales[LAST][:, BLK:], h_last[:, BLK * PACK :])
         y_bank = second_layer(LAST, BLK, C, 2)
-        nc.vector.tensor_copy(scattered(LAST, 0, BLK), y_last[0][:])
-        nc.scalar.activation(y_last[1][:], y_bank[:], COPY)
-        nc.vector.tensor_tensor(scattered(LAST, BLK, C), y_last[1][:], gate_sb[LAST][:, BLK:], MULT)
+        nc.scalar.activation(scattered(LAST, 0, BLK), y_last[0][:], COPY)
+        nc.vector.tensor_tensor(y_last[1][:], y_bank[:], gate_sb[LAST][:, BLK:], MULT)
+        nc.vector.tensor_copy(scattered(LAST, BLK, C), y_last[1][:])
 
-        for lo in range(0, T, T // 4):
-            cols = slice(lo, lo + T // 4)
-            out_sb = sbuf(f"out{lo}", [P, T // 4], F32)
-            nc.vector.tensor_tensor(out_sb[:], window[:, cols], xr_sb[:, cols], ADD)
-            (nc.sync, nc.scalar)[lo // (T // 4) % 2].dma_start(out[:, cols], out_sb[:])
+        for piece, (lo, hi) in enumerate(zip(CUTS, CUTS[1:])):
+            out_sb = sbuf(f"out{lo}", [P, hi - lo], F32)
+            nc.vector.tensor_tensor(out_sb[:], window[:, lo:hi], xr_sb[:, lo:hi], ADD)
+            (nc.sync, nc.scalar)[piece % 2].dma_start(out[:, lo:hi], out_sb[:])

@@ -27,7 +27,7 @@ W_SHARE_SIXTH = 60
 END = H * PACK // 2
 LAP = 64
 
-CUTS = (0, 128, 320, 640, T)
+CUTS = (0, T // 4, T // 2, 3 * T // 4, T)
 
 F32 = mybir.dt.float32
 BF16 = mybir.dt.bfloat16
@@ -241,9 +241,8 @@ def tile_moe_res_glu_relu_kernel(tc, xT, xr, w1, w3, w2, gate, offs, out):
         for t in (1, 0):
             cols = slice(t * P, (t + 1) * P)
             quantize(w_codes[end][:, cols], w_scales[end][:, cols], end_lower[:, t * P * PACK : (t + 1) * P * PACK])
-        products(LAST, W3, 1, 0, b_last[0], (3, 2))
         y_bank = second_layer(FIRST, 0, C, 4)
-        products(LAST, W3, 1, 0, b_last[0], (1, 0))
+        products(LAST, W3, 1, 0, b_last[0], (3, 2, 1, 0))
         products(LAST, W3, 1, 1, b_last[1], (3, 2, 1, 0))
         cast_rows(w2_bf[LAST], w2_raw[LAST], N // 4)
         y_first = sbuf("y_first", [P, C], F32)

@@ -261,7 +261,7 @@ def tile_moe_res_glu_relu_kernel(tc, xT, xr, w1, w3, w2, gate, offs, out):
         nc.vector.tensor_tensor(y_last[1][:], y_bank[:], gate_sb[LAST][:, BLK:], MULT)
         nc.vector.tensor_copy(scattered(LAST, BLK, C), y_last[1][:])
 
-        for piece, (lo, hi) in enumerate(zip(CUTS, CUTS[1:])):
+        for lo, hi in zip(CUTS, CUTS[1:]):
             out_sb = sbuf(f"out{lo}", [P, hi - lo], F32)
             nc.vector.tensor_tensor(out_sb[:], window[:, lo:hi], xr_sb[:, lo:hi], ADD)
-            (nc.sync, nc.scalar)[piece % 2].dma_start(out[:, lo:hi], out_sb[:])
+            nc.sync.dma_start(out[:, lo:hi], out_sb[:])

@@ -19,10 +19,10 @@ FIRST, LAST = 0, 1
 X_SHARE = 104
 W_SHARE = 80
 W_SHARE_URGENT = 48
-W_SHARE_RELUS = 56
+W_SHARE_RELUS = 64
 W_SHARE_GATHER = 104
 W_SHARE_LATE = 70
-W_SHARE_SIXTH = 60
+W_SHARE_SIXTH = 66
 
 END = H * PACK // 2
 LAP = 64
@@ -201,7 +201,7 @@ def tile_moe_res_glu_relu_kernel(tc, xT, xr, w1, w3, w2, gate, offs, out):
         cast_chunk((FIRST, W1, 0), W_SHARE_GATHER)
         gather_words(1)
         nc.vector.tensor_copy(slot_bytes[:], x_bytes[:].indirect(offsets[:]))
-        cast_chunk((FIRST, W1, 1), W_SHARE)
+        cast_chunk((FIRST, W1, 1), W_SHARE_GATHER)
         for s in range(PASSES):
             quantize_chunk((FIRST, W1, s))
         a_first = first_layer(FIRST, W1, (0, 1))

@@ -19,10 +19,10 @@ FIRST, LAST = 0, 1
 X_SHARE = 104
 W_SHARE = 80
 W_SHARE_URGENT = 48
-W_SHARE_RELUS = 64
+W_SHARE_RELUS = 68
 W_SHARE_GATHER = 104
-W_SHARE_LATE = 70
-W_SHARE_SIXTH = 66
+W_SHARE_LATE = 76
+W_SHARE_SIXTH = 72
 
 END = H * PACK // 2
 LAP = 64

from contextlib import ExitStack

import concourse.mybir as mybir

K, T, E, C, H, N = 1024, 1024, 2, 256, 512, 128
S = E * C
FLOPS = 2 * S * (2 * K * H + H * N)

P = 128
PACK = 4
K_PASS = P * PACK
PASSES = K // K_PASS
BLK = 128
BLOCKS = C // BLK
HALF = T // 2
W1, W3 = 0, 1
FIRST, LAST = 0, 1

X_SHARE = 104
W_SHARE = 80
W_SHARE_URGENT = 48
W_SHARE_RELUS = 68
W_SHARE_GATHER = 104
W_SHARE_LATE = 76
W_SHARE_SIXTH = 72

END = H * PACK // 2
LAP = 64

CUTS = (0, T // 4, T // 2, 3 * T // 4, T)

F32 = mybir.dt.float32
BF16 = mybir.dt.bfloat16
U32 = mybir.dt.uint32
U16 = mybir.dt.uint16
U8 = mybir.dt.uint8
FP8X4 = mybir.dt.float8_e4m3fn_x4
COPY = mybir.ActivationFunctionType.Copy
RELU = mybir.ActivationFunctionType.Relu
MULT = mybir.AluOpType.mult
ADD = mybir.AluOpType.add


def tile_moe_res_glu_relu_kernel(tc, xT, xr, w1, w3, w2, gate, offs, out):
    nc = tc.nc
    with ExitStack() as ctx:
        keep = ctx.enter_context(tc.tile_pool(name="keep", bufs=1))
        psum = ctx.enter_context(tc.psum_pool(name="psum", bufs=1))

        def sbuf(name, shape, dtype):
            return keep.tile(shape, dtype, name=name, tag=name, align_bytes=256)

        def bank_tile(number, shape):
            return psum.tile(shape, F32, name=f"bank{number}", tag=f"bank{number}")

        chunks = [(e, g, s) for e in range(E) for g in (W1, W3) for s in range(PASSES)]
        end = chunks[-1]

        offsets = keep.tile([P, S // 16], U16, name="offsets")
        x_raw = [sbuf(f"x_raw{s}", [P, PACK, T], F32) for s in range(PASSES)]
        x_bf = [sbuf(f"x_bf{s}", [P, T * PACK], BF16) for s in range(PASSES)]
        x_words = [sbuf(f"x_words{s}", [P, T], U32) for s in range(PASSES)]
        x_bytes = sbuf("x_bytes", [P, T], U8)
        slot_words = [sbuf(f"slot_words{s}", [P, S], U32) for s in range(PASSES)]
        slot_bytes = sbuf("slot_bytes", [P, S], U8)
        w_raw = {c: sbuf("w_raw%d%d%d" % c, [P, PACK, H], F32)[:] for c in chunks if c[:2] != (LAST, W1)}
        h_start = PACK * H - LAP
        h_stop = h_start + C * PACK // 2
        shared = sbuf("shared", [P, h_stop - LAP + PACK * H], F32)
        w_raw[LAST, W1, 0] = shared[:, : PACK * H].rearrange("p (j w) -> p j w", j=PACK)
        w_raw[LAST, W1, 1] = shared[:, h_stop - LAP :].rearrange("p (j w) -> p j w", j=PACK)
        h_first = shared[:, h_start:h_stop].bitcast(BF16)
        w_bf = {c: sbuf("w_bf%d%d%d" % c, [P, H * PACK], BF16) for c in chunks[:-1]}
        w_codes = {c: sbuf("w_codes%d%d%d" % c, [P, H], U32) for c in chunks}
        w_scales = {c: sbuf("w_scales%d%d%d" % c, [P, H], U8) for c in chunks}
        w2_raw = [sbuf(f"w2_raw{e}", [P, PACK, N], F32) for e in range(E)]
        end_upper = sbuf("end_upper", [P, END], BF16)[:]
        end_lower = sbuf("end_lower", [P, END], BF16)[:]
        h_last = sbuf("h_last", [P, C * PACK], BF16)
        w2_bf = [sbuf("w2_bf0", [P, N * PACK], BF16)[:], h_last[:, BLK * PACK :]]
        w2_codes = [sbuf(f"w2_codes{e}", [P, N], U32) for e in range(E)]
        w2_scales = [sbuf("w2_scales0", [P, N], U8)[:], w_scales[end][4:P, :N]]
        h_codes = [sbuf(f"h_codes{e}", [P, C], U32) for e in range(E)]
        h_scales = [sbuf(f"h_scales{e}", [P, C], U8) for e in range(E)]
        gate_sb = [sbuf(f"gate{e}", [P, C], F32) for e in range(E)]
        xr_sb = sbuf("xr", [P, T], F32)
        window = sbuf("window", [P, T], F32)

        nc.gpsimd.memset(x_bytes[:], 0)
        nc.gpsimd.memset(window[:], 0.0)

        def load_rows(tile, rows):
            nc.sync.dma_start(tile, rows.rearrange("(p j) w -> p j w", j=PACK))

        def load_chunk(e, g, s):
            load_rows(w_raw[e, g, s], (w1, w3)[g][e][s * K_PASS : (s + 1) * K_PASS, :])

        nc.sync.dma_start(offsets[:], offs)
        load_rows(x_raw[0][:], xT[:K_PASS, :])
        load_rows(x_raw[1][:], xT[K_PASS:, :])
        for c in chunks:
            load_chunk(*c)
        for e in range(E):
            load_rows(w2_raw[e][:], w2[e])
            nc.sync.dma_start(gate_sb[e][:], gate[:, e * C : (e + 1) * C])
        nc.sync.dma_start(xr_sb[:], xr)

        def cast(dst, src, share):
            if share > 0:
                nc.scalar.activation(dst[:, :share], src[:, :share], COPY)
            if share < dst.shape[1]:
                nc.vector.tensor_copy(dst[:, share:], src[:, share:])

        def cast_rows(bf, raw, share):
            cast(
                bf.rearrange("p (c i j) -> p c j i", i=4, j=PACK),
                raw[:].rearrange("p j (c i) -> p c j i", i=4),
                share,
            )

        def cast_chunk(c, share):
            cast(
                w_bf[c][:].rearrange("p (t m j) -> p m j t", t=PACK, j=PACK),
                w_raw[c].rearrange("p j (m t) -> p m j t", t=PACK),
                share,
            )

        def quantize(codes, scales, values):
            nc.vector.quantize_mx(out=codes.bitcast(FP8X4), scales=scales, in_=values)

        def quantize_chunk(c):
            quantize(w_codes[c][:], w_scales[c][:], w_bf[c][:])

        def quantize_tokens(s):
            dst = x_bf[s][:].rearrange("p (c i j) -> p c j i", i=4, j=PACK)
            src = x_raw[s][:].rearrange("p j (c i) -> p c j i", i=4)
            nc.vector.tensor_copy(dst[:, HALF // 4 :], src[:, HALF // 4 :])
            cast(dst[:, : HALF // 4], src[:, : HALF // 4], X_SHARE)
            for lo in (HALF, 0):
                cols = slice(lo, lo + HALF)
                quantize(x_words[s][:, cols], x_bytes[4 * s : P, cols], x_bf[s][:, lo * PACK : (lo + HALF) * PACK])

        def gather_words(s):
            nc.vector.tensor_copy(slot_words[s][:], x_words[s][:].indirect(offsets[:]))

        def products(e, g, s, b, bank, t_order):
            slots = slice(e * C + b * BLK, e * C + (b + 1) * BLK)
            for t in t_order:
                cols = slice(t * P, (t + 1) * P)
                nc.tensor.matmul_mx(
                    out=bank[:, t, :],
                    lhsT=w_codes[e, g, s][:, cols].bitcast(FP8X4),
                    lhsT_scale=w_scales[e, g, s][:, cols],
                    rhs=slot_words[s][:, slots].bitcast(FP8X4),
                    rhs_scale=slot_bytes[4 * s : P, slots],
                    start=(s == 0 and t == PACK - 1),
                    stop=(s == PASSES - 1 and t == 0),
                )

        def first_layer(e, g, bank_numbers, passes=PASSES):
            banks = [bank_tile(number, [P, PACK, BLK]) for number in bank_numbers]
            for s in range(passes):
                for b in range(BLOCKS):
                    products(e, g, s, b, banks[b], (3, 2, 1, 0))
            return banks

        def by_slot(bank):
            return bank[:].rearrange("p t (r n) -> p r n t", r=4)

        def in_runs(flat):
            return flat.rearrange("p (r n t) -> p r n t", r=4, t=PACK)

        def cast_part(c, lo=0):
            return w_raw[c][:, :, lo : lo + BLK].rearrange("p r (n t) -> p r n t", t=PACK)

        def relu(dst, bank):
            nc.scalar.activation(dst, by_slot(bank), RELU)

        def gated(h_bf, bank, relu_values):
            nc.vector.tensor_tensor(in_runs(h_bf), by_slot(bank), relu_values, MULT)

        def second_layer(e, lo, hi, bank_number):
            bank = bank_tile(bank_number, [P, hi - lo])
            nc.tensor.matmul_mx(
                out=bank[:],
                lhsT=w2_codes[e][:].bitcast(FP8X4),
                lhsT_scale=w2_scales[e],
                rhs=h_codes[e][:, lo:hi].bitcast(FP8X4),
                rhs_scale=h_scales[e][:, lo:hi],
                start=True,
                stop=True,
            )
            return bank

        def scattered(e, lo, hi):
            return window[:].indirect(offsets[:, (e * C + lo) // 16 : (e * C + hi) // 16])

        quantize_tokens(0)
        gather_words(0)
        quantize_tokens(1)
        cast_chunk((FIRST, W1, 0), W_SHARE_GATHER)
        gather_words(1)
        nc.vector.tensor_copy(slot_bytes[:], x_bytes[:].indirect(offsets[:]))
        cast_chunk((FIRST, W1, 1), W_SHARE_GATHER)
        for s in range(PASSES):
            quantize_chunk((FIRST, W1, s))
        a_first = first_layer(FIRST, W1, (0, 1))
        cast_chunk((FIRST, W3, 0), W_SHARE)
        quantize_chunk((FIRST, W3, 0))
        cast_chunk((FIRST, W3, 1), W_SHARE_URGENT)
        quantize_chunk((FIRST, W3, 1))
        relu_first = [cast_part((FIRST, W3, 1), lo) for lo in (0, H - BLK)]
        for b in range(BLOCKS):
            relu(relu_first[b], a_first[b])
        b_first = first_layer(FIRST, W3, (2, 3))

        cast_chunk((LAST, W1, 0), W_SHARE_LATE)
        gated(h_first[:, : BLK * PACK], b_first[0], relu_first[0])
        quantize_chunk((LAST, W1, 0))
        dst = w_bf[LAST, W1, 1][:].rearrange("p (t m j) -> p m j t", t=PACK, j=PACK)
        src = w_raw[LAST, W1, 1].rearrange("p j (m t) -> p m j t", t=PACK)
        nc.vector.tensor_copy(dst[:, : P - W_SHARE_SIXTH], src[:, : P - W_SHARE_SIXTH])
        nc.scalar.activation(dst[:, P - W_SHARE_SIXTH :], src[:, P - W_SHARE_SIXTH :], COPY)
        gated(h_first[:, BLK * PACK :], b_first[1], relu_first[1])
        quantize_chunk((LAST, W1, 1))
        quantize(h_codes[FIRST][:], h_scales[FIRST][:], h_first)
        a_last = first_layer(LAST, W1, (5, 6))
        cast_chunk((LAST, W3, 0), W_SHARE_RELUS)
        quantize_chunk((LAST, W3, 0))
        relu_last = [cast_part((LAST, W3, 0)), w2_raw[FIRST][:].rearrange("p r (n t) -> p r n t", t=PACK)]
        relu(relu_last[0], a_last[0])

        b_last = first_layer(LAST, W3, (7, 0), 1)
        end_src = w_raw[end].rearrange("p j (m t) -> p m j t", t=PACK)
        cast(end_upper.rearrange("p (t m j) -> p m j t", t=2, j=PACK), end_src[:, :, :, 2:], 0)
        cast(end_lower.rearrange("p (t m j) -> p m j t", t=2, j=PACK), end_src[:, :, :, :2], P)
        cast_rows(w2_bf[FIRST], w2_raw[FIRST], 0)
        relu(relu_last[1], a_last[1])
        quantize(w_codes[end][:, H // 2 :], w_scales[end][:, H // 2 :], end_upper)
        quantize(w2_codes[FIRST][:], w2_scales[FIRST], w2_bf[FIRST])
        for t in (1, 0):
            cols = slice(t * P, (t + 1) * P)
            quantize(w_codes[end][:, cols], w_scales[end][:, cols], end_lower[:, t * P * PACK : (t + 1) * P * PACK])
        y_bank = second_layer(FIRST, 0, C, 4)
        products(LAST, W3, 1, 0, b_last[0], (3, 2, 1, 0))
        products(LAST, W3, 1, 1, b_last[1], (3, 2, 1, 0))
        cast_rows(w2_bf[LAST], w2_raw[LAST], N // 4)
        y_first = sbuf("y_first", [P, C], F32)
        y_last = [sbuf(f"y_last{b}", [P, BLK], F32) for b in range(BLOCKS)]
        nc.vector.tensor_tensor(y_first[:], y_bank[:], gate_sb[FIRST][:], MULT)
        nc.scalar.activation(scattered(FIRST, 0, C), y_first[:], COPY)
        gated(h_last[:, : BLK * PACK], b_last[0], relu_last[0])
        quantize(w2_codes[LAST][:], w2_scales[LAST], w2_bf[LAST])
        quantize(h_codes[LAST][:, :BLK], h_scales[LAST][:, :BLK], h_last[:, : BLK * PACK])
        y_bank = second_layer(LAST, 0, BLK, 1)
        gated(h_last[:, BLK * PACK :], b_last[1], relu_last[1])
        nc.vector.tensor_tensor(y_last[0][:], y_bank[:], gate_sb[LAST][:, :BLK], MULT)
        quantize(h_codes[LAST][:, BLK:], h_scales[LAST][:, BLK:], h_last[:, BLK * PACK :])
        y_bank = second_layer(LAST, BLK, C, 2)
        nc.scalar.activation(scattered(LAST, 0, BLK), y_last[0][:], COPY)
        nc.vector.tensor_tensor(y_last[1][:], y_bank[:], gate_sb[LAST][:, BLK:], MULT)
        nc.vector.tensor_copy(scattered(LAST, BLK, C), y_last[1][:])

        for lo, hi in zip(CUTS, CUTS[1:]):
            out_sb = sbuf(f"out{lo}", [P, hi - lo], F32)
            nc.vector.tensor_tensor(out_sb[:], window[:, lo:hi], xr_sb[:, lo:hi], ADD)
            nc.sync.dma_start(out[:, lo:hi], out_sb[:])
